import numpy as np
import ml_dtypes


def mxq(x, axis, fmt="e4m3"):
    dtype, down = {"e4m3": (ml_dtypes.float8_e4m3fn, 7), "e5m2": (ml_dtypes.float8_e5m2, 14)}[fmt]
    v = np.moveaxis(np.asarray(x, np.float32).astype(ml_dtypes.bfloat16).astype(np.float64), axis, -1)
    blocks = v.reshape(v.shape[:-1] + (-1, 32))
    amax = np.abs(blocks).max(-1, keepdims=True)
    byte = np.maximum(np.where(amax > 0, np.frexp(amax)[1] - 1 + 127, 0) - down, 1)
    scale = np.exp2(byte - 127.0)
    codes = (blocks / scale).astype(np.float32).astype(dtype).astype(np.float64)
    return np.moveaxis((codes * scale).reshape(v.shape), -1, axis)


WIDE = False


def mx_kscale(k):
    if not WIDE:
        return np.ones(k)
    levels = np.array([10, -10, 5, -5, 0])
    if k % 512:
        return np.exp2(np.random.permutation(np.resize(levels, k // 32))).repeat(32)
    a = np.empty((k // 512, 16))
    for p in range(k // 512):
        a[p, :8] = np.random.permutation(np.resize(levels, 8))
        for g in range(8):
            far = levels[np.abs(levels - a[p, g]) >= 10]
            a[p, g + 8] = far[np.random.randint(len(far))]
    return np.exp2(a.ravel()).repeat(32)


def f64(x):
    return np.asarray(x).astype(np.float64)


def striped(idx):
    return np.tile(np.asarray(idx).reshape(-1, 16).T, (8, 1)).astype(np.uint16)


def unstriped(offs):
    return offs[:16].T.reshape(-1).astype(np.int64)


E2M1 = np.array([0.0, 0.5, 1.0, 1.5, 2.0, 3.0, 4.0, 6.0, -0.0, -0.5, -1.0, -1.5, -2.0, -3.0, -4.0, -6.0])


def pack_weight(w, fmt):
    k, n = w.shape
    w = f64(np.asarray(w, np.float32).astype(ml_dtypes.bfloat16)).reshape(k // 32, 32, n)
    amax = np.abs(w).max(1)
    if fmt == "e4m3":
        byte = np.frexp(amax)[1] - 1 + 127 - 7
    else:
        mant, ex = np.frexp(amax / 6.0)
        byte = np.where(mant > 0.5, ex, ex - 1) + 127
    byte = np.clip(np.where(amax > 0, byte, 1), 1, 254)
    scaled = (w * np.exp2(127.0 - byte)[:, None, :]).reshape(k, n).astype(np.float32)
    by_word = np.ascontiguousarray(scaled.reshape(k // 512, 128, 4, n).transpose(0, 1, 3, 2))
    if fmt == "e4m3":
        words = by_word.astype(ml_dtypes.float8_e4m3fn).view(np.uint8)
    else:
        c = by_word.astype(ml_dtypes.float4_e2m1fn).view(np.uint8) & 0xF
        words = (c[..., 0::2] | (c[..., 1::2] << 4)).reshape(k // 512, 128, 2 * n)
    return np.ascontiguousarray(words), np.ascontiguousarray(byte.astype(np.uint8).reshape(k // 512, 16, n))


def unpack_weight(words, scales, fmt):
    g, _, n = scales.shape
    words = np.ascontiguousarray(words).reshape(g, 128, n, -1)
    if fmt == "e4m3":
        vals = words.view(ml_dtypes.float8_e4m3fn).astype(np.float64)
    else:
        nib = np.empty((g, 128, n, 4), np.uint8)
        nib[..., 0::2] = words & 0xF
        nib[..., 1::2] = words >> 4
        vals = E2M1[nib]
    vals = vals * np.repeat(np.exp2(scales.astype(np.float64) - 127.0), 8, axis=1)[..., None]
    return vals.transpose(0, 1, 3, 2).reshape(g * 512, n)


def sigmoid(v):
    return 1.0 / (1.0 + np.exp(-v))


D, T, I, Q, E, G, M = 512, 1024, 512, 512, 512, 64, 1024


def setup_inputs():
    n = np.random.standard_normal
    idx = np.random.permutation(T)[:I]
    idx2 = np.random.permutation(T)[:I]
    idx3 = np.random.permutation(T)[:I]
    idx4 = np.random.permutation(M)[:I]
    fd = mx_kscale(D)
    fq = mx_kscale(Q)
    keysp = pack_weight(n((D, T)) / fd[:, None], "e2m1")
    return {
        "query": (n((D, Q)) * 1.2 / np.sqrt(D) * fd[:, None]).astype(np.float32),
        "keys_words": keysp[0],
        "keys_scales": keysp[1],
        "lam": (np.random.uniform(0.5, 1.5, (Q, 1))).astype(np.float32),
        "cap": (np.random.uniform(0.01, 0.018, (Q, 1))).astype(np.float32),
        "qs": (np.random.uniform(20.0, 80.0, (Q, 1)) * fq[:, None]).astype(np.float32),
        "msgs": (n((Q, E)) * 1 / np.sqrt(Q) / fq[:, None]).astype(np.float32),
        "old": (n((E, M)) * 1.0).astype(np.float32),
        "fade": (np.random.uniform(0.3, 0.9, (1, M))).astype(np.float32),
        "offs": striped(idx),
        "offs2": striped(idx2),
        "offs3": striped(idx3),
        "offs4": striped(idx4),
    }


def reference(query, keys_words, keys_scales, lam, cap, qs, msgs, old, fade, offs, offs2, offs3, offs4):
    idx = unstriped(offs)
    idx2 = unstriped(offs2)
    idx3 = unstriped(offs3)
    idx4 = unstriped(offs4)
    keysu = unpack_weight(keys_words, keys_scales, "e2m1")
    queryq = mxq(f64(query), 0, "e4m3")
    a = queryq.T @ keysu
    g1 = sigmoid(a[:, idx2] * 2.0)
    s = (a[:, idx] * g1 + a[:, idx3] * (1.0 - g1)) * f64(lam)
    p = np.exp(s - np.max(s, axis=1, keepdims=True))
    r = p / np.sum(p, axis=1, keepdims=True)
    pg = r.reshape(Q, G, I // G).sum(axis=2)
    k0 = np.minimum(pg, f64(cap)) / pg
    kr = np.repeat(k0, I // G, axis=1)
    w = r * kr
    wq = w * f64(qs)
    msgsq = mxq(f64(msgs), 0, "e4m3")
    wqq = mxq(wq, 0, "e4m3")
    dl = msgsq.T @ wqq
    df = np.zeros((E, M))
    df[:, idx4] = dl
    y = f64(old) * f64(fade) + df
    return y

@@ -1,0 +1,306 @@
+from contextlib import ExitStack
+
+import concourse.mybir as mybir
+
+D, T, I, Q, E, G, M = 512, 1024, 512, 512, 512, 64, 1024
+FLOPS = 2 * D * Q * T + 2 * Q * E * I
+
+F32 = mybir.dt.float32
+BF16 = mybir.dt.bfloat16
+I32 = mybir.dt.int32
+U32 = mybir.dt.uint32
+U16 = mybir.dt.uint16
+U8 = mybir.dt.uint8
+FP8X4 = mybir.dt.float8_e4m3fn_x4
+FP4X4 = mybir.dt.float4_e2m1fn_x4
+ALU = mybir.AluOpType
+ACT = mybir.ActivationFunctionType
+AXIS = mybir.AxisListType
+
+P = 128
+PACK = 4
+BANK = 512
+RUN = I // G
+HALF = I // 2
+TINY = 1e-30
+
+
+def tile_attend_conditioned_runcap_delivered_kernel(
+    tc, query, keys_words, keys_scales, lam, cap, qs, msgs, old, fade, offs, offs2, offs3, offs4, out
+):
+    nc = tc.nc
+    with ExitStack() as ctx:
+        keep = ctx.enter_context(tc.tile_pool(name="keep", bufs=1))
+        psum = ctx.enter_context(tc.psum_pool(name="psum", bufs=1))
+
+        def sb(name, shape, dtype=F32, tag=None):
+            return keep.tile(shape, dtype, name=name, tag=tag or name, align_bytes=64)
+
+        def bank(b):
+            return psum.tile([P, BANK], F32, name=f"bank{b}")
+
+        query_rows = query.rearrange("(p t) q -> p t q", t=PACK)
+        query_raw = []
+        for h in range(2):
+            raw = sb(f"query_raw{h}", [P, PACK, Q // 2])
+            nc.sync.dma_start(out=raw[:], in_=query_rows[:, :, h * (Q // 2) : (h + 1) * (Q // 2)])
+            query_raw.append(raw)
+        scale_rows = sb("scale_rows", [4, 4, T // 4], I32)
+        nc.scalar.dma_start(out=scale_rows[:], in_=keys_scales[0].bitcast(I32).rearrange("(u f) c -> f u c", f=4))
+        key_words = sb("key_words", [P, 2 * T], U8)
+        nc.sync.dma_start(out=key_words[:], in_=keys_words[0])
+        lists = {}
+        for name, src in (("second", offs3), ("first", offs), ("judge", offs2)):
+            lists[name] = keep.tile([P, I // 16], U16, name=f"list_{name}")
+            nc.sync.dma_start(lists[name][:], src)
+        row_factor = {}
+        for name, src in (("lam", lam), ("cap", cap), ("qs", qs)):
+            row_factor[name] = sb(f"row_{name}", [P, PACK])
+            nc.sync.dma_start(out=row_factor[name][:], in_=src.rearrange("(p r) o -> p (r o)", r=PACK))
+        old_tiles = [sb(f"old{j}", [P, M]) for j in range(4)]
+        msgs_raw = sb("msgs_raw", [P, PACK, E])
+        nc.sync.dma_start(out=msgs_raw[:], in_=msgs.rearrange("(p t) e -> p t e", t=PACK))
+        lists["places"] = keep.tile([P, I // 16], U16, name="list_places")
+        nc.sync.dma_start(lists["places"][:], offs4)
+        fade_all = sb("fade_all", [P, M])
+        nc.sync.dma_start(out=fade_all[:], in_=fade[0].partition_broadcast(P))
+        fade_row = fade_all[:]
+        for j in range(4):
+            nc.sync.dma_start(out=old_tiles[j][:], in_=old[j * P : (j + 1) * P, :])
+
+        key_scales = sb("key_scales", [P, T // 4], I32)
+        nc.vector.memset(key_scales[:], 0)
+        for u in range(4):
+            nc.vector.tensor_copy(out=key_scales[32 * u : 32 * u + 4, :], in_=scale_rows[:, u, :])
+        windows = [sb(f"window{j}", [P, M]) for j in range(4)]
+        for j in range(4):
+            nc.vector.memset(windows[j][:], 0.0)
+
+        query_bf = sb("query_bf", [P, PACK, P, PACK], BF16)
+        for h in range(2):
+            nc.vector.tensor_copy(
+                out=query_bf[:, :, 64 * h : 64 * (h + 1), :].rearrange("p r s t -> p s r t"),
+                in_=query_raw[h][:].rearrange("p t (s r) -> p s r t", r=PACK),
+            )
+        query_codes = sb("query_codes", [P, Q], U32)
+        query_scales = sb("query_scales", [P, Q], U8)
+        products = [sb(f"products{r}", [P, T]) for r in range(PACK)]
+        score_banks = {}
+        for r in range(PACK):
+            cols = slice(r * P, (r + 1) * P)
+            nc.vector.quantize_mx(
+                out=query_codes[:, cols].bitcast(FP8X4),
+                scales=query_scales[:, cols],
+                in_=query_bf[:, r, :, :].rearrange("p s t -> p (s t)"),
+            )
+        for r in range(PACK):
+            cols = slice(r * P, (r + 1) * P)
+            for h in range(2):
+                acc = bank(2 * r + h)
+                nc.tensor.matmul_mx(
+                    out=acc[:],
+                    lhsT=query_codes[:, cols].bitcast(FP8X4),
+                    lhsT_scale=query_scales[:, cols],
+                    rhs=key_words[:, h * 2 * BANK : (h + 1) * 2 * BANK].bitcast(FP4X4),
+                    rhs_scale=key_scales[:].bitcast(U8)[:, h * BANK : (h + 1) * BANK],
+                    start=True,
+                    stop=True,
+                )
+                score_banks[r, h] = acc
+
+        cap_floor = sb("cap_floor", [P, PACK])
+        cap_qs = sb("cap_qs", [P, PACK])
+        weights_bf = sb("weights_bf", [P, PACK, I], BF16)
+        tiles = {}
+
+        def empty_scores(r, h, engine):
+            dst = products[r][:, h * BANK : (h + 1) * BANK]
+            if engine == "S":
+                nc.scalar.activation(out=dst, in_=score_banks[r, h][:], func=ACT.Copy)
+            else:
+                nc.vector.tensor_copy(out=dst, in_=score_banks[r, h][:])
+
+        def look_second(r):
+            tiles["second", r] = sb(f"second{r}", [P, I])
+            nc.scalar.activation(out=tiles["second", r][:], in_=products[r][:].indirect(lists["second"][:]), func=ACT.Copy)
+
+        def look_judge(r):
+            looked = sb(f"judge_product{r}", [P, I])
+            nc.scalar.activation(out=looked[:], in_=products[r][:].indirect(lists["judge"][:]), func=ACT.Copy)
+            tiles["judge", r] = sb(f"judge{r}", [P, I])
+            nc.scalar.activation(out=tiles["judge", r][:], in_=looked[:], func=ACT.Tanh)
+
+        def look_first(r):
+            tiles["first", r] = sb(f"first{r}", [P, I])
+            nc.scalar.activation(out=tiles["first", r][:], in_=products[r][:].indirect(lists["first"][:]), func=ACT.Copy)
+
+        def difference(r):
+            tiles["score", r] = sb(f"score{r}", [P, I])
+            if ("first", r) in tiles:
+                first = tiles["first", r][:]
+            else:
+                first = products[r][:].indirect(lists["first"][:])
+            nc.vector.tensor_tensor(out=tiles["score", r][:], in0=first, in1=tiles["second", r][:], op=ALU.subtract)
+
+        def score(r):
+            s = tiles["score", r]
+            nc.vector.scalar_tensor_tensor(
+                out=s[:], in0=tiles["judge", r][:], scalar=1.0, in1=s[:], op0=ALU.add, op1=ALU.mult
+            )
+            nc.vector.scalar_tensor_tensor(
+                out=s[:], in0=s[:], scalar=-0.5, in1=tiles["second", r][:], op0=ALU.mult, op1=ALU.subtract
+            )
+            tiles["neg_max", r] = sb(f"neg_max{r}", [P, 1])
+            nc.vector.tensor_scalar(
+                out=s[:], in0=s[:], scalar1=row_factor["lam"][:, r : r + 1], scalar2=None,
+                op0=ALU.mult, op1=ALU.min, accum_out=tiles["neg_max", r][:],
+            )
+
+        def exponent(r):
+            tiles["p", r] = sb(f"p{r}", [P, G, RUN])
+            tiles["row_sum", r] = sb(f"row_sum{r}", [P, 1])
+            nc.scalar.activation(
+                out=tiles["p", r][:].rearrange("p g j -> p (g j)"), in_=tiles["score", r][:], func=ACT.Exp,
+                bias=tiles["neg_max", r][:], scale=-1.0, accum_out=tiles["row_sum", r][:],
+            )
+
+        def weigh(r):
+            p = tiles["p", r]
+            run_sum = sb(f"run_sum{r}", [P, G])
+            nc.vector.tensor_reduce(out=run_sum[:], in_=p[:], axis=AXIS.X, op=ALU.add)
+            nc.vector.scalar_tensor_tensor(
+                out=run_sum[:], in0=cap_floor[:, r : r + 1].to_broadcast([P, G]), scalar=tiles["row_sum", r][:],
+                in1=run_sum[:], op0=ALU.mult, op1=ALU.max,
+            )
+            inverse = sb(f"inverse{r}", [P, G])
+            nc.vector.reciprocal(out=inverse[:], in_=run_sum[:])
+            nc.vector.scalar_tensor_tensor(
+                out=weights_bf[:, r, :].rearrange("p (g j) -> p g j", j=RUN), in0=p[:], scalar=cap_qs[:, r : r + 1],
+                in1=inverse[:].unsqueeze(2).to_broadcast([P, G, RUN]), op0=ALU.mult, op1=ALU.mult,
+            )
+
+        def fade_old(j, engine):
+            engine.tensor_tensor(out=tiles["faded"][:, j, :], in0=old_tiles[j][:], in1=fade_row, op=ALU.mult)
+
+        msgs_codes = sb("msgs_codes", [P, E], U32)
+        msgs_scales = sb("msgs_scales", [P, E], U8)
+
+        def weave_msgs():
+            msgs_bf = sb("msgs_bf", [P, E, PACK], BF16, tag="judge_product3")
+            tiles["msgs_bf"] = msgs_bf
+            nc.scalar.copy(
+                out=msgs_bf[:].rearrange("p (c i) t -> p c t i", i=4),
+                in_=msgs_raw[:].rearrange("p t (c i) -> p c t i", i=4),
+            )
+
+        def quantize_msgs():
+            nc.vector.quantize_mx(
+                out=msgs_codes[:].bitcast(FP8X4), scales=msgs_scales[:], in_=tiles["msgs_bf"][:].rearrange("p e t -> p (e t)")
+            )
+
+        def row_constants():
+            nc.vector.tensor_scalar(
+                out=cap_floor[:], in0=row_factor["cap"][:], scalar1=TINY, scalar2=None, op0=ALU.max
+            )
+            nc.vector.tensor_tensor(out=cap_qs[:], in0=row_factor["cap"][:], in1=row_factor["qs"][:], op=ALU.mult)
+
+        empty_scores(0, 0, "S")
+        empty_scores(0, 1, "V")
+        look_second(0)
+        look_judge(0)
+        empty_scores(1, 0, "V")
+        empty_scores(1, 1, "V")
+        difference(0)
+        row_constants()
+        look_second(1)
+        look_judge(1)
+        score(0)
+        difference(1)
+        exponent(0)
+        empty_scores(2, 0, "S")
+        empty_scores(2, 1, "S")
+        look_second(2)
+        look_judge(2)
+        score(1)
+        weigh(0)
+        exponent(1)
+        difference(2)
+        empty_scores(3, 0, "S")
+        empty_scores(3, 1, "S")
+        look_second(3)
+        look_judge(3)
+        score(2)
+        weigh(1)
+        exponent(2)
+        difference(3)
+        score(3)
+        exponent(3)
+        weigh(2)
+        weave_msgs()
+        quantize_msgs()
+        weigh(3)
+
+        woven = [sb(f"woven{h}", [P, HALF, PACK], BF16) for h in range(2)]
+        weight_codes = [sb(f"weight_codes{h}", [P, HALF], U32) for h in range(2)]
+        weight_scales = [sb(f"weight_scales{h}", [P, HALF], U8) for h in range(2)]
+        for h in range(2):
+            dst = woven[h][:].rearrange("p (c i) r -> p c r i", i=4)
+            src = weights_bf[:, :, h * HALF : (h + 1) * HALF].rearrange("p r (c i) -> p c r i", i=4)
+            if h == 0:
+                nc.vector.tensor_copy(out=dst, in_=src)
+            else:
+                nc.scalar.copy(out=dst, in_=src)
+        tiles["faded"] = sb("faded", [P, 4, M], tag="weights_bf")
+        sums = {}
+        for h in range(2):
+            nc.vector.quantize_mx(
+                out=weight_codes[h][:].bitcast(FP8X4), scales=weight_scales[h][:],
+                in_=woven[h][:].rearrange("p i r -> p (i r)"),
+            )
+            for j in range(4):
+                acc = bank(4 * h + j)
+                cols = slice(j * P, (j + 1) * P)
+                nc.tensor.matmul_mx(
+                    out=acc[:, :HALF],
+                    lhsT=msgs_codes[:, cols].bitcast(FP8X4),
+                    lhsT_scale=msgs_scales[:, cols],
+                    rhs=weight_codes[h][:].bitcast(FP8X4),
+                    rhs_scale=weight_scales[h][:],
+                    start=True,
+                    stop=True,
+                )
+                sums[j, h] = acc
+
+        def deliver(j, h, engine):
+            staged = sb(f"staged{j}_{h}", [P, HALF])
+            places = windows[j][:].indirect(lists["places"][:, 16 * h : 16 * (h + 1)])
+            if engine == "S":
+                nc.scalar.copy(out=staged[:], in_=sums[j, h][:, :HALF])
+                nc.scalar.activation(out=places, in_=staged[:], func=ACT.Copy)
+            else:
+                nc.vector.tensor_copy(out=staged[:], in_=sums[j, h][:, :HALF])
+                nc.vector.tensor_copy(out=places, in_=staged[:])
+
+        def finish(j, engine, pieces=1):
+            width = M // pieces
+            for k in range(pieces):
+                cols = slice(k * width, (k + 1) * width)
+                engine.tensor_tensor(out=old_tiles[j][:, cols], in0=tiles["faded"][:, j, cols], in1=windows[j][:, cols], op=ALU.add)
+                nc.sync.dma_start(out=out[j * P : (j + 1) * P, cols], in_=old_tiles[j][:, cols])
+
+        deliver(0, 0, "S")
+        deliver(3, 0, "V")
+        deliver(0, 1, "S")
+        deliver(3, 1, "V")
+        deliver(1, 0, "S")
+        fade_old(3, nc.vector)
+        finish(3, nc.vector)
+        deliver(1, 1, "S")
+        fade_old(0, nc.vector)
+        finish(0, nc.vector)
+        deliver(2, 0, "S")
+        fade_old(1, nc.vector)
+        finish(1, nc.vector)
+        deliver(2, 1, "S")
+        fade_old(2, nc.vector)
+        finish(2, nc.vector, 2)

@@ -1,6 +1,7 @@
 from contextlib import ExitStack
 
 import concourse.mybir as mybir
+from concourse.masks import make_identity
 
 D, T, I, Q, E, G, M = 512, 1024, 512, 512, 512, 64, 1024
 FLOPS = 2 * D * Q * T + 2 * Q * E * I
@@ -21,8 +22,10 @@ P = 128
 PACK = 4
 BANK = 512
 RUN = I // G
-HALF = I // 2
+PIECES = (slice(0, 128), slice(128, I))
 TINY = 1e-30
+EARLY = 5
+QPARTS = 4
 
 
 def tile_attend_conditioned_runcap_delivered_kernel(
@@ -39,34 +42,39 @@ def tile_attend_conditioned_runcap_delivered_kernel(
         def bank(b):
             return psum.tile([P, BANK], F32, name=f"bank{b}")
 
+        scale_rows = sb("scale_rows", [4, 4, T // 4], I32)
+        nc.sync.dma_start(out=scale_rows[:], in_=keys_scales[0].bitcast(I32).rearrange("(u f) c -> f u c", f=4))
         query_rows = query.rearrange("(p t) q -> p t q", t=PACK)
         query_raw = []
-        for h in range(2):
-            raw = sb(f"query_raw{h}", [P, PACK, Q // 2])
-            nc.sync.dma_start(out=raw[:], in_=query_rows[:, :, h * (Q // 2) : (h + 1) * (Q // 2)])
+        part = Q // QPARTS
+        for h in range(QPARTS):
+            raw = sb(f"query_raw{h}", [P, PACK, part])
+            nc.sync.dma_start(out=raw[:], in_=query_rows[:, :, h * part : (h + 1) * part])
             query_raw.append(raw)
-        scale_rows = sb("scale_rows", [4, 4, T // 4], I32)
-        nc.scalar.dma_start(out=scale_rows[:], in_=keys_scales[0].bitcast(I32).rearrange("(u f) c -> f u c", f=4))
         key_words = sb("key_words", [P, 2 * T], U8)
         nc.sync.dma_start(out=key_words[:], in_=keys_words[0])
         lists = {}
-        for name, src in (("second", offs3), ("first", offs), ("judge", offs2)):
+        for name, src in (("second", offs3), ("judge", offs2), ("first", offs)):
             lists[name] = keep.tile([P, I // 16], U16, name=f"list_{name}")
             nc.sync.dma_start(lists[name][:], src)
+        lam_cols = [sb(f"lam{r}", [P, 1]) for r in range(PACK)]
+        with nc.allow_non_contiguous_dma(reason="one factor to a partition"):
+            for r in range(PACK):
+                nc.sync.dma_start(out=lam_cols[r][:], in_=lam.rearrange("(p r) o -> r p o", r=PACK)[r])
         row_factor = {}
-        for name, src in (("lam", lam), ("cap", cap), ("qs", qs)):
+        for name, src in (("cap", cap), ("qs", qs)):
             row_factor[name] = sb(f"row_{name}", [P, PACK])
             nc.sync.dma_start(out=row_factor[name][:], in_=src.rearrange("(p r) o -> p (r o)", r=PACK))
-        old_tiles = [sb(f"old{j}", [P, M]) for j in range(4)]
         msgs_raw = sb("msgs_raw", [P, PACK, E])
         nc.sync.dma_start(out=msgs_raw[:], in_=msgs.rearrange("(p t) e -> p t e", t=PACK))
         lists["places"] = keep.tile([P, I // 16], U16, name="list_places")
         nc.sync.dma_start(lists["places"][:], offs4)
-        fade_all = sb("fade_all", [P, M])
-        nc.sync.dma_start(out=fade_all[:], in_=fade[0].partition_broadcast(P))
-        fade_row = fade_all[:]
+        old_tiles = [sb(f"old{j}", [P, M]) for j in range(4)]
         for j in range(4):
             nc.sync.dma_start(out=old_tiles[j][:], in_=old[j * P : (j + 1) * P, :])
+        fade_cols = sb("fade_cols", [P, M // P])
+        with nc.allow_non_contiguous_dma(reason="one fading value to a partition"):
+            nc.sync.dma_start(out=fade_cols[:], in_=fade.rearrange("o (b p) -> p (o b)", p=P))
 
         key_scales = sb("key_scales", [P, T // 4], I32)
         nc.vector.memset(key_scales[:], 0)
@@ -74,17 +82,19 @@ def tile_attend_conditioned_runcap_delivered_kernel(
             nc.vector.tensor_copy(out=key_scales[32 * u : 32 * u + 4, :], in_=scale_rows[:, u, :])
         windows = [sb(f"window{j}", [P, M]) for j in range(4)]
         for j in range(4):
-            nc.vector.memset(windows[j][:], 0.0)
+            (nc.vector if j < 2 else nc.gpsimd).memset(windows[j][:], 0.0)
+        identity = sb("identity", [P, P])
+        make_identity(nc, identity[:])
 
         query_bf = sb("query_bf", [P, PACK, P, PACK], BF16)
-        for h in range(2):
+        rows = P // QPARTS
+        for h in range(QPARTS):
             nc.vector.tensor_copy(
-                out=query_bf[:, :, 64 * h : 64 * (h + 1), :].rearrange("p r s t -> p s r t"),
+                out=query_bf[:, :, rows * h : rows * (h + 1), :].rearrange("p r s t -> p s r t"),
                 in_=query_raw[h][:].rearrange("p t (s r) -> p s r t", r=PACK),
             )
         query_codes = sb("query_codes", [P, Q], U32)
         query_scales = sb("query_scales", [P, Q], U8)
-        products = [sb(f"products{r}", [P, T]) for r in range(PACK)]
         score_banks = {}
         for r in range(PACK):
             cols = slice(r * P, (r + 1) * P)
@@ -113,46 +123,57 @@ def tile_attend_conditioned_runcap_delivered_kernel(
         weights_bf = sb("weights_bf", [P, PACK, I], BF16)
         tiles = {}
 
-        def empty_scores(r, h, engine):
-            dst = products[r][:, h * BANK : (h + 1) * BANK]
+        def empty_scores(r, h, engine, after=None):
+            if h == 0:
+                tiles["products", r] = sb(f"products{r}", [P, T], tag=f"score{r - 2}" if r >= 2 else None)
+            dst = tiles["products", r][:, h * BANK : (h + 1) * BANK]
             if engine == "S":
                 nc.scalar.activation(out=dst, in_=score_banks[r, h][:], func=ACT.Copy)
             else:
                 nc.vector.tensor_copy(out=dst, in_=score_banks[r, h][:])
 
-        def look_second(r):
+        def look_second(r, engine="S"):
             tiles["second", r] = sb(f"second{r}", [P, I])
-            nc.scalar.activation(out=tiles["second", r][:], in_=products[r][:].indirect(lists["second"][:]), func=ACT.Copy)
+            looked = tiles["products", r][:].indirect(lists["second"][:])
+            if engine == "S":
+                nc.scalar.activation(out=tiles["second", r][:], in_=looked, func=ACT.Copy)
+            else:
+                nc.vector.tensor_copy(out=tiles["second", r][:], in_=looked)
 
         def look_judge(r):
-            looked = sb(f"judge_product{r}", [P, I])
-            nc.scalar.activation(out=looked[:], in_=products[r][:].indirect(lists["judge"][:]), func=ACT.Copy)
-            tiles["judge", r] = sb(f"judge{r}", [P, I])
-            nc.scalar.activation(out=tiles["judge", r][:], in_=looked[:], func=ACT.Tanh)
+            tiles["judge_product", r] = sb(f"judge_product{r}", [P, I])
+            nc.scalar.activation(
+                out=tiles["judge_product", r][:], in_=tiles["products", r][:].indirect(lists["judge"][:]), func=ACT.Copy
+            )
 
-        def look_first(r):
-            tiles["first", r] = sb(f"first{r}", [P, I])
-            nc.scalar.activation(out=tiles["first", r][:], in_=products[r][:].indirect(lists["first"][:]), func=ACT.Copy)
+        def squash(r, after=None):
+            tiles["judge", r] = sb(f"judge{r}", [P, I], tag=f"lam{r - 1}" if r >= 1 else None)
+            nc.scalar.activation(out=tiles["judge", r][:], in_=tiles["judge_product", r][:], func=ACT.Tanh)
 
-        def difference(r):
-            tiles["score", r] = sb(f"score{r}", [P, I])
-            if ("first", r) in tiles:
-                first = tiles["first", r][:]
-            else:
-                first = products[r][:].indirect(lists["first"][:])
-            nc.vector.tensor_tensor(out=tiles["score", r][:], in0=first, in1=tiles["second", r][:], op=ALU.subtract)
+        def difference(r, after=None):
+            tiles["mixed", r] = sb(f"mixed{r}", [P, I], tag="mixed")
+            nc.vector.tensor_tensor(
+                out=tiles["mixed", r][:], in0=tiles["products", r][:].indirect(lists["first"][:]),
+                in1=tiles["second", r][:], op=ALU.subtract,
+            )
 
-        def score(r):
-            s = tiles["score", r]
+        def mix(r):
+            s = tiles["mixed", r]
             nc.vector.scalar_tensor_tensor(
                 out=s[:], in0=tiles["judge", r][:], scalar=1.0, in1=s[:], op0=ALU.add, op1=ALU.mult
             )
+
+        def blend(r):
+            s = tiles["mixed", r]
             nc.vector.scalar_tensor_tensor(
                 out=s[:], in0=s[:], scalar=-0.5, in1=tiles["second", r][:], op0=ALU.mult, op1=ALU.subtract
             )
+
+        def peak(r):
+            tiles["score", r] = sb(f"score{r}", [P, I])
             tiles["neg_max", r] = sb(f"neg_max{r}", [P, 1])
             nc.vector.tensor_scalar(
-                out=s[:], in0=s[:], scalar1=row_factor["lam"][:, r : r + 1], scalar2=None,
+                out=tiles["score", r][:], in0=tiles["mixed", r][:], scalar1=lam_cols[r][:], scalar2=None,
                 op0=ALU.mult, op1=ALU.min, accum_out=tiles["neg_max", r][:],
             )
 
@@ -164,38 +185,46 @@ def tile_attend_conditioned_runcap_delivered_kernel(
                 bias=tiles["neg_max", r][:], scale=-1.0, accum_out=tiles["row_sum", r][:],
             )
 
-        def weigh(r):
-            p = tiles["p", r]
-            run_sum = sb(f"run_sum{r}", [P, G])
-            nc.vector.tensor_reduce(out=run_sum[:], in_=p[:], axis=AXIS.X, op=ALU.add)
+        def run_sums(r):
+            tiles["run_sum", r] = sb(f"run_sum{r}", [P, G])
+            nc.vector.tensor_reduce(out=tiles["run_sum", r][:], in_=tiles["p", r][:], axis=AXIS.X, op=ALU.add)
+
+        def clamp(r):
+            run_sum = tiles["run_sum", r]
             nc.vector.scalar_tensor_tensor(
                 out=run_sum[:], in0=cap_floor[:, r : r + 1].to_broadcast([P, G]), scalar=tiles["row_sum", r][:],
                 in1=run_sum[:], op0=ALU.mult, op1=ALU.max,
             )
-            inverse = sb(f"inverse{r}", [P, G])
-            nc.vector.reciprocal(out=inverse[:], in_=run_sum[:])
+
+        def invert(r, slots=slice(0, I)):
+            if slots.start == 0:
+                tiles["inverse", r] = sb(f"inverse{r}", [P, G])
+            runs = slice(slots.start // RUN, slots.stop // RUN)
+            nc.vector.reciprocal(out=tiles["inverse", r][:, runs], in_=tiles["run_sum", r][:, runs])
+
+        def final(r, slots=slice(0, I)):
+            runs = slice(slots.start // RUN, slots.stop // RUN)
+            count = runs.stop - runs.start
             nc.vector.scalar_tensor_tensor(
-                out=weights_bf[:, r, :].rearrange("p (g j) -> p g j", j=RUN), in0=p[:], scalar=cap_qs[:, r : r + 1],
-                in1=inverse[:].unsqueeze(2).to_broadcast([P, G, RUN]), op0=ALU.mult, op1=ALU.mult,
+                out=weights_bf[:, r, slots].rearrange("p (g j) -> p g j", j=RUN), in0=tiles["p", r][:, runs, :],
+                scalar=cap_qs[:, r : r + 1],
+                in1=tiles["inverse", r][:, runs].unsqueeze(2).to_broadcast([P, count, RUN]), op0=ALU.mult, op1=ALU.mult,
             )
 
-        def fade_old(j, engine):
-            engine.tensor_tensor(out=tiles["faded"][:, j, :], in0=old_tiles[j][:], in1=fade_row, op=ALU.mult)
+        msgs_codes = [sb(f"msgs_codes{h}", [P, E // 2], U32) for h in range(2)]
+        msgs_scales = [sb(f"msgs_scales{h}", [P, E // 2], U8) for h in range(2)]
 
-        msgs_codes = sb("msgs_codes", [P, E], U32)
-        msgs_scales = sb("msgs_scales", [P, E], U8)
-
-        def weave_msgs():
-            msgs_bf = sb("msgs_bf", [P, E, PACK], BF16, tag="judge_product3")
-            tiles["msgs_bf"] = msgs_bf
+        def weave_msgs(h, after=None):
+            tiles["msgs_bf", h] = sb(f"msgs_bf{h}", [P, E // 2, PACK], BF16, tag=("score2", "neg_max3")[h])
             nc.scalar.copy(
-                out=msgs_bf[:].rearrange("p (c i) t -> p c t i", i=4),
-                in_=msgs_raw[:].rearrange("p t (c i) -> p c t i", i=4),
+                out=tiles["msgs_bf", h][:].rearrange("p (c i) t -> p c t i", i=4),
+                in_=msgs_raw[:, :, h * (E // 2) : (h + 1) * (E // 2)].rearrange("p t (c i) -> p c t i", i=4),
             )
 
-        def quantize_msgs():
+        def quantize_msgs(h):
             nc.vector.quantize_mx(
-                out=msgs_codes[:].bitcast(FP8X4), scales=msgs_scales[:], in_=tiles["msgs_bf"][:].rearrange("p e t -> p (e t)")
+                out=msgs_codes[h][:].bitcast(FP8X4), scales=msgs_scales[h][:],
+                in_=tiles["msgs_bf", h][:].rearrange("p e t -> p (e t)"),
             )
 
         def row_constants():
@@ -204,103 +233,175 @@ def tile_attend_conditioned_runcap_delivered_kernel(
             )
             nc.vector.tensor_tensor(out=cap_qs[:], in0=row_factor["cap"][:], in1=row_factor["qs"][:], op=ALU.mult)
 
+        def fade_turned(b, after=None):
+            if b == 0:
+                early = sb("faded_early", [P, EARLY, E], tag="judge_product3")
+                late = sb("faded_late", [P, M // P - EARLY, E], tag="score3")
+                tiles["faded"] = [early[:, k, :] for k in range(EARLY)] + [late[:, k, :] for k in range(M // P - EARLY)]
+            turned = bank(b)
+            for j in range(4):
+                nc.tensor.transpose(turned[:, j * P : (j + 1) * P], old_tiles[j][:, b * P : (b + 1) * P], identity[:])
+            nc.scalar.activation(out=tiles["faded"][b], in_=turned[:], func=ACT.Copy, scale=fade_cols[:, b : b + 1])
+
         empty_scores(0, 0, "S")
         empty_scores(0, 1, "V")
-        look_second(0)
         look_judge(0)
-        empty_scores(1, 0, "V")
-        empty_scores(1, 1, "V")
-        difference(0)
+        look_second(0, "V")
+        squash(0)
         row_constants()
-        look_second(1)
-        look_judge(1)
-        score(0)
-        difference(1)
+        difference(0)
+        mix(0)
+        blend(0)
+        peak(0)
         exponent(0)
-        empty_scores(2, 0, "S")
-        empty_scores(2, 1, "S")
-        look_second(2)
-        look_judge(2)
-        score(1)
-        weigh(0)
+        empty_scores(1, 0, "S")
+        empty_scores(1, 1, "S")
+        look_judge(1)
+        look_second(1)
+        squash(1, "m0")
+        difference(1, "m0")
+        run_sums(0)
+        mix(1)
+        clamp(0)
+        blend(1)
+        invert(0)
+        peak(1)
+        final(0)
         exponent(1)
-        difference(2)
-        empty_scores(3, 0, "S")
-        empty_scores(3, 1, "S")
-        look_second(3)
-        look_judge(3)
-        score(2)
-        weigh(1)
+        empty_scores(2, 0, "S", "x0")
+        empty_scores(2, 1, "S", "x0")
+        look_judge(2)
+        look_second(2)
+        squash(2, "m1")
+        difference(2, "m1")
+        run_sums(1)
+        mix(2)
+        clamp(1)
+        blend(2)
+        invert(1)
+        peak(2)
+        final(1)
         exponent(2)
-        difference(3)
-        score(3)
+        empty_scores(3, 0, "S", "x1")
+        empty_scores(3, 1, "S", "x1")
+        look_judge(3)
+        look_second(3)
+        squash(3, "m2")
+        difference(3, "m2")
+        run_sums(2)
+        mix(3)
+        clamp(2)
+        blend(3)
+        invert(2)
+        peak(3)
+        final(2)
         exponent(3)
-        weigh(2)
-        weave_msgs()
-        quantize_msgs()
-        weigh(3)
+        run_sums(3)
+        clamp(3)
+        invert(3, PIECES[0])
+        invert(3, PIECES[1])
+        final(3, PIECES[0])
+        final(3, PIECES[1])
+        weave_msgs(0, "x2")
+        quantize_msgs(0)
+        weave_msgs(1, "x3")
+        quantize_msgs(1)
+        fade_turned(0, "t3")
+        fade_turned(1, "t3")
+        fade_turned(2, "t3")
+        fade_turned(3, "t3")
+        fade_turned(4, "t3")
+        fade_turned(5, "x3")
+        fade_turned(6, "x3")
+        fade_turned(7, "x3")
 
-        woven = [sb(f"woven{h}", [P, HALF, PACK], BF16) for h in range(2)]
-        weight_codes = [sb(f"weight_codes{h}", [P, HALF], U32) for h in range(2)]
-        weight_scales = [sb(f"weight_scales{h}", [P, HALF], U8) for h in range(2)]
-        for h in range(2):
-            dst = woven[h][:].rearrange("p (c i) r -> p c r i", i=4)
-            src = weights_bf[:, :, h * HALF : (h + 1) * HALF].rearrange("p r (c i) -> p c r i", i=4)
-            if h == 0:
+        widths = [piece.stop - piece.start for piece in PIECES]
+        woven = [sb(f"woven{h}", [P, widths[h], PACK], BF16) for h in range(2)]
+        weight_codes = [sb(f"weight_codes{h}", [P, widths[h]], U32) for h in range(2)]
+        weight_scales = [sb(f"weight_scales{h}", [P, widths[h]], U8) for h in range(2)]
+        for h, lo, hi, engine in ((0, 0, 128, "V"), (1, 128, 256, "V"), (1, 256, I, "S")):
+            base = PIECES[h].start
+            dst = woven[h][:, lo - base : hi - base, :].rearrange("p (c i) r -> p c r i", i=4)
+            src = weights_bf[:, :, lo:hi].rearrange("p r (c i) -> p c r i", i=4)
+            if engine == "V":
                 nc.vector.tensor_copy(out=dst, in_=src)
             else:
                 nc.scalar.copy(out=dst, in_=src)
-        tiles["faded"] = sb("faded", [P, 4, M], tag="weights_bf")
         sums = {}
-        for h in range(2):
+
+        def quantize_weights(h):
             nc.vector.quantize_mx(
                 out=weight_codes[h][:].bitcast(FP8X4), scales=weight_scales[h][:],
                 in_=woven[h][:].rearrange("p i r -> p (i r)"),
             )
-            for j in range(4):
-                acc = bank(4 * h + j)
-                cols = slice(j * P, (j + 1) * P)
+
+        def multiply(j, h, b):
+            acc = bank(b)
+            cols = slice((j % 2) * P, (j % 2 + 1) * P)
+            for part_cols in ((slice(0, 128),), (slice(0, 128), slice(128, 384)))[h]:
                 nc.tensor.matmul_mx(
-                    out=acc[:, :HALF],
-                    lhsT=msgs_codes[:, cols].bitcast(FP8X4),
-                    lhsT_scale=msgs_scales[:, cols],
-                    rhs=weight_codes[h][:].bitcast(FP8X4),
-                    rhs_scale=weight_scales[h][:],
+                    out=acc[:, part_cols],
+                    lhsT=msgs_codes[j // 2][:, cols].bitcast(FP8X4),
+                    lhsT_scale=msgs_scales[j // 2][:, cols],
+                    rhs=weight_codes[h][:, part_cols].bitcast(FP8X4),
+                    rhs_scale=weight_scales[h][:, part_cols],
                     start=True,
                     stop=True,
                 )
-                sums[j, h] = acc
+            sums[j, h] = acc
 
-        def deliver(j, h, engine):
-            staged = sb(f"staged{j}_{h}", [P, HALF])
-            places = windows[j][:].indirect(lists["places"][:, 16 * h : 16 * (h + 1)])
+        def stage(j, h, engine):
+            tiles["staged", j, h] = sb(f"staged{j}_{h}", [P, widths[h]])
             if engine == "S":
-                nc.scalar.copy(out=staged[:], in_=sums[j, h][:, :HALF])
-                nc.scalar.activation(out=places, in_=staged[:], func=ACT.Copy)
+                nc.scalar.copy(out=tiles["staged", j, h][:], in_=sums[j, h][:, : widths[h]])
             else:
-                nc.vector.tensor_copy(out=staged[:], in_=sums[j, h][:, :HALF])
-                nc.vector.tensor_copy(out=places, in_=staged[:])
+                nc.vector.tensor_copy(out=tiles["staged", j, h][:], in_=sums[j, h][:, : widths[h]])
 
-        def finish(j, engine, pieces=1):
-            width = M // pieces
-            for k in range(pieces):
-                cols = slice(k * width, (k + 1) * width)
-                engine.tensor_tensor(out=old_tiles[j][:, cols], in0=tiles["faded"][:, j, cols], in1=windows[j][:, cols], op=ALU.add)
+        def scatter(j, h, engine):
+            places = windows[j][:].indirect(lists["places"][:, PIECES[h].start // 16 : PIECES[h].stop // 16])
+            if engine == "S":
+                nc.scalar.activation(out=places, in_=tiles["staged", j, h][:], func=ACT.Copy)
+            else:
+                nc.vector.tensor_copy(out=places, in_=tiles["staged", j, h][:])
+
+        def finish(j, b0, b1):
+            for k, b in enumerate((b0, b1)):
+                back = bank(b)
+                for c in range(4):
+                    nc.tensor.transpose(
+                        back[:, c * P : (c + 1) * P], tiles["faded"][4 * k + c][:, j * P : (j + 1) * P], identity[:]
+                    )
+                cols = slice(k * BANK, (k + 1) * BANK)
+                nc.vector.tensor_tensor(out=old_tiles[j][:, cols], in0=back[:], in1=windows[j][:, cols], op=ALU.add)
                 nc.sync.dma_start(out=out[j * P : (j + 1) * P, cols], in_=old_tiles[j][:, cols])
 
-        deliver(0, 0, "S")
-        deliver(3, 0, "V")
-        deliver(0, 1, "S")
-        deliver(3, 1, "V")
-        deliver(1, 0, "S")
-        fade_old(3, nc.vector)
-        finish(3, nc.vector)
-        deliver(1, 1, "S")
-        fade_old(0, nc.vector)
-        finish(0, nc.vector)
-        deliver(2, 0, "S")
-        fade_old(1, nc.vector)
-        finish(1, nc.vector)
-        deliver(2, 1, "S")
-        fade_old(2, nc.vector)
-        finish(2, nc.vector, 2)
+        quantize_weights(0)
+        multiply(0, 0, 0)
+        multiply(1, 0, 1)
+        multiply(2, 0, 3)
+        stage(0, 0, "V")
+        scatter(0, 0, "S")
+        quantize_weights(1)
+        stage(1, 0, "V")
+        stage(2, 0, "V")
+        multiply(0, 1, 2)
+        multiply(3, 1, 0)
+        multiply(1, 1, 4)
+        multiply(2, 1, 5)
+        scatter(1, 0, "S")
+        stage(0, 1, "V")
+        scatter(0, 1, "S")
+        scatter(2, 0, "V")
+        stage(3, 1, "V")
+        multiply(3, 0, 2)
+        stage(1, 1, "V")
+        stage(3, 0, "V")
+        scatter(3, 1, "V")
+        scatter(3, 0, "V")
+        scatter(1, 1, "S")
+        stage(2, 1, "S")
+        scatter(2, 1, "S")
+        finish(0, 6, 7)
+        finish(3, 4, 2)
+        finish(1, 6, 7)
+        finish(2, 3, 5)

@@ -25,7 +25,6 @@ RUN = I // G
 PIECES = (slice(0, 128), slice(128, I))
 TINY = 1e-30
 EARLY = 5
-QPARTS = 4
 
 
 def tile_attend_conditioned_runcap_delivered_kernel(
@@ -42,15 +41,13 @@ def tile_attend_conditioned_runcap_delivered_kernel(
         def bank(b):
             return psum.tile([P, BANK], F32, name=f"bank{b}")
 
-        scale_rows = sb("scale_rows", [4, 4, T // 4], I32)
-        nc.sync.dma_start(out=scale_rows[:], in_=keys_scales[0].bitcast(I32).rearrange("(u f) c -> f u c", f=4))
-        query_rows = query.rearrange("(p t) q -> p t q", t=PACK)
-        query_raw = []
-        part = Q // QPARTS
-        for h in range(QPARTS):
-            raw = sb(f"query_raw{h}", [P, PACK, part])
-            nc.sync.dma_start(out=raw[:], in_=query_rows[:, :, h * part : (h + 1) * part])
-            query_raw.append(raw)
+        key_scales = sb("key_scales", [P, T // 4], I32)
+        nc.gpsimd.memset(key_scales[:], 0)
+        query_raw = sb("query_raw", [P, PACK, Q])
+        nc.sync.dma_start(out=query_raw[:], in_=query.rearrange("(p t) q -> p t q", t=PACK))
+        scale_rows = keys_scales[0].bitcast(I32)
+        for u in range(4):
+            nc.sync.dma_start(out=key_scales[32 * u : 32 * u + 4, :], in_=scale_rows[4 * u : 4 * u + 4, :])
         key_words = sb("key_words", [P, 2 * T], U8)
         nc.sync.dma_start(out=key_words[:], in_=keys_words[0])
         lists = {}
@@ -76,35 +73,28 @@ def tile_attend_conditioned_runcap_delivered_kernel(
         with nc.allow_non_contiguous_dma(reason="one fading value to a partition"):
             nc.sync.dma_start(out=fade_cols[:], in_=fade.rearrange("o (b p) -> p (o b)", p=P))
 
-        key_scales = sb("key_scales", [P, T // 4], I32)
-        nc.vector.memset(key_scales[:], 0)
-        for u in range(4):
-            nc.vector.tensor_copy(out=key_scales[32 * u : 32 * u + 4, :], in_=scale_rows[:, u, :])
         windows = [sb(f"window{j}", [P, M]) for j in range(4)]
         for j in range(4):
-            (nc.vector if j < 2 else nc.gpsimd).memset(windows[j][:], 0.0)
+            (nc.vector if j < 4 else nc.gpsimd).memset(windows[j][:], 0.0)
         identity = sb("identity", [P, P])
         make_identity(nc, identity[:])
 
-        query_bf = sb("query_bf", [P, PACK, P, PACK], BF16)
-        rows = P // QPARTS
-        for h in range(QPARTS):
-            nc.vector.tensor_copy(
-                out=query_bf[:, :, rows * h : rows * (h + 1), :].rearrange("p r s t -> p s r t"),
-                in_=query_raw[h][:].rearrange("p t (s r) -> p s r t", r=PACK),
-            )
         query_codes = sb("query_codes", [P, Q], U32)
         query_scales = sb("query_scales", [P, Q], U8)
         score_banks = {}
+        query_dealt = query_raw[:].rearrange("p t (s r) -> p r s t", r=PACK)
         for r in range(PACK):
             cols = slice(r * P, (r + 1) * P)
+            query_bf = sb(f"query_bf{r}", [P, P, PACK], BF16)
+            if r == 1:
+                nc.scalar.copy(out=query_bf[:], in_=query_dealt[:, r, :, :])
+            else:
+                nc.vector.tensor_copy(out=query_bf[:], in_=query_dealt[:, r, :, :])
             nc.vector.quantize_mx(
                 out=query_codes[:, cols].bitcast(FP8X4),
                 scales=query_scales[:, cols],
-                in_=query_bf[:, r, :, :].rearrange("p s t -> p (s t)"),
+                in_=query_bf[:].rearrange("p s t -> p (s t)"),
             )
-        for r in range(PACK):
-            cols = slice(r * P, (r + 1) * P)
             for h in range(2):
                 acc = bank(2 * r + h)
                 nc.tensor.matmul_mx(
@@ -364,36 +354,35 @@ def tile_attend_conditioned_runcap_delivered_kernel(
             else:
                 nc.vector.tensor_copy(out=places, in_=tiles["staged", j, h][:])
 
-        def finish(j, b0, b1):
-            for k, b in enumerate((b0, b1)):
-                back = bank(b)
-                for c in range(4):
-                    nc.tensor.transpose(
-                        back[:, c * P : (c + 1) * P], tiles["faded"][4 * k + c][:, j * P : (j + 1) * P], identity[:]
-                    )
-                cols = slice(k * BANK, (k + 1) * BANK)
-                nc.vector.tensor_tensor(out=old_tiles[j][:, cols], in0=back[:], in1=windows[j][:, cols], op=ALU.add)
-                nc.sync.dma_start(out=out[j * P : (j + 1) * P, cols], in_=old_tiles[j][:, cols])
+        def finish(j, k, b):
+            back = bank(b)
+            for c in range(4):
+                nc.tensor.transpose(
+                    back[:, c * P : (c + 1) * P], tiles["faded"][4 * k + c][:, j * P : (j + 1) * P], identity[:]
+                )
+            cols = slice(k * BANK, (k + 1) * BANK)
+            nc.vector.tensor_tensor(out=old_tiles[j][:, cols], in0=back[:], in1=windows[j][:, cols], op=ALU.add)
+            nc.sync.dma_start(out=out[j * P : (j + 1) * P, cols], in_=old_tiles[j][:, cols])
 
         quantize_weights(0)
-        multiply(0, 0, 0)
-        multiply(1, 0, 1)
-        multiply(2, 0, 3)
+        multiply(0, 0, 4)
+        multiply(1, 0, 5)
+        multiply(2, 0, 6)
         stage(0, 0, "V")
         scatter(0, 0, "S")
         quantize_weights(1)
         stage(1, 0, "V")
         stage(2, 0, "V")
-        multiply(0, 1, 2)
-        multiply(3, 1, 0)
-        multiply(1, 1, 4)
-        multiply(2, 1, 5)
+        multiply(0, 1, 4)
+        multiply(3, 1, 7)
+        multiply(1, 1, 5)
+        multiply(2, 1, 6)
         scatter(1, 0, "S")
         stage(0, 1, "V")
         scatter(0, 1, "S")
         scatter(2, 0, "V")
         stage(3, 1, "V")
-        multiply(3, 0, 2)
+        multiply(3, 0, 7)
         stage(1, 1, "V")
         stage(3, 0, "V")
         scatter(3, 1, "V")
@@ -401,7 +390,11 @@ def tile_attend_conditioned_runcap_delivered_kernel(
         scatter(1, 1, "S")
         stage(2, 1, "S")
         scatter(2, 1, "S")
-        finish(0, 6, 7)
-        finish(3, 4, 2)
-        finish(1, 6, 7)
-        finish(2, 3, 5)
+        finish(0, 0, 0)
+        finish(0, 1, 4)
+        finish(3, 0, 3)
+        finish(3, 1, 7)
+        finish(1, 0, 1)
+        finish(1, 1, 5)
+        finish(2, 0, 2)
+        finish(2, 1, 6)

@@ -95,32 +95,42 @@ def tile_attend_conditioned_runcap_delivered_kernel(
                 scales=query_scales[:, cols],
                 in_=query_bf[:].rearrange("p s t -> p (s t)"),
             )
-            for h in range(2):
-                acc = bank(2 * r + h)
+            banks = (0, 1, 6, 7) if r == 0 else (2 * r, 2 * r + 1)
+            width = T // len(banks)
+            for h, b in enumerate(banks):
+                acc = bank(b)
                 nc.tensor.matmul_mx(
-                    out=acc[:],
+                    out=acc[:, :width],
                     lhsT=query_codes[:, cols].bitcast(FP8X4),
                     lhsT_scale=query_scales[:, cols],
-                    rhs=key_words[:, h * 2 * BANK : (h + 1) * 2 * BANK].bitcast(FP4X4),
-                    rhs_scale=key_scales[:].bitcast(U8)[:, h * BANK : (h + 1) * BANK],
+                    rhs=key_words[:, h * 2 * width : (h + 1) * 2 * width].bitcast(FP4X4),
+                    rhs_scale=key_scales[:].bitcast(U8)[:, h * width : (h + 1) * width],
                     start=True,
                     stop=True,
                 )
-                score_banks[r, h] = acc
+                score_banks[r, h] = acc[:, :width]
+            if r == 0:
+                first_products = sb("products0", [P, T])
+                for h in range(4):
+                    dst = first_products[:, h * width : (h + 1) * width]
+                    if h % 2 == 0:
+                        nc.scalar.activation(out=dst, in_=score_banks[0, h], func=ACT.Copy)
+                    else:
+                        nc.vector.tensor_copy(out=dst, in_=score_banks[0, h])
 
         cap_floor = sb("cap_floor", [P, PACK])
         cap_qs = sb("cap_qs", [P, PACK])
         weights_bf = sb("weights_bf", [P, PACK, I], BF16)
-        tiles = {}
+        tiles = {("products", 0): first_products}
 
         def empty_scores(r, h, engine, after=None):
             if h == 0:
                 tiles["products", r] = sb(f"products{r}", [P, T], tag=f"score{r - 2}" if r >= 2 else None)
             dst = tiles["products", r][:, h * BANK : (h + 1) * BANK]
             if engine == "S":
-                nc.scalar.activation(out=dst, in_=score_banks[r, h][:], func=ACT.Copy)
+                nc.scalar.activation(out=dst, in_=score_banks[r, h], func=ACT.Copy)
             else:
-                nc.vector.tensor_copy(out=dst, in_=score_banks[r, h][:])
+                nc.vector.tensor_copy(out=dst, in_=score_banks[r, h])
 
         def look_second(r, engine="S"):
             tiles["second", r] = sb(f"second{r}", [P, I])
@@ -233,8 +243,6 @@ def tile_attend_conditioned_runcap_delivered_kernel(
                 nc.tensor.transpose(turned[:, j * P : (j + 1) * P], old_tiles[j][:, b * P : (b + 1) * P], identity[:])
             nc.scalar.activation(out=tiles["faded"][b], in_=turned[:], func=ACT.Copy, scale=fade_cols[:, b : b + 1])
 
-        empty_scores(0, 0, "S")
-        empty_scores(0, 1, "V")
         look_judge(0)
         look_second(0, "V")
         squash(0)
@@ -354,15 +362,19 @@ def tile_attend_conditioned_runcap_delivered_kernel(
             else:
                 nc.vector.tensor_copy(out=places, in_=tiles["staged", j, h][:])
 
-        def finish(j, k, b):
+        def finish(j, k, b, pieces=1):
             back = bank(b)
             for c in range(4):
                 nc.tensor.transpose(
                     back[:, c * P : (c + 1) * P], tiles["faded"][4 * k + c][:, j * P : (j + 1) * P], identity[:]
                 )
-            cols = slice(k * BANK, (k + 1) * BANK)
-            nc.vector.tensor_tensor(out=old_tiles[j][:, cols], in0=back[:], in1=windows[j][:, cols], op=ALU.add)
-            nc.sync.dma_start(out=out[j * P : (j + 1) * P, cols], in_=old_tiles[j][:, cols])
+            width = BANK // pieces
+            for n in range(pieces):
+                cols = slice(k * BANK + n * width, k * BANK + (n + 1) * width)
+                nc.vector.tensor_tensor(
+                    out=old_tiles[j][:, cols], in0=back[:, n * width : (n + 1) * width], in1=windows[j][:, cols], op=ALU.add
+                )
+                nc.sync.dma_start(out=out[j * P : (j + 1) * P, cols], in_=old_tiles[j][:, cols])
 
         quantize_weights(0)
         multiply(0, 0, 4)
@@ -397,4 +409,4 @@ def tile_attend_conditioned_runcap_delivered_kernel(
         finish(1, 0, 1)
         finish(1, 1, 5)
         finish(2, 0, 2)
-        finish(2, 1, 6)
+        finish(2, 1, 6, 2)

@@ -19,12 +19,21 @@ ACT = mybir.ActivationFunctionType
 AXIS = mybir.AxisListType
 
 P = 128
+SCALAR, VECTOR = "scalar", "vector"
 PACK = 4
 BANK = 512
 RUN = I // G
-PIECES = (slice(0, 128), slice(128, I))
+TILES = E // P
+BLOCKS = M // P
+LAST = PACK - 1
+LINE = 4
+ENTRIES = 16
 TINY = 1e-30
-EARLY = 5
+
+SHORT, LONG = 0, 1
+PIECES = (slice(0, 128), slice(128, I))
+WEAVE_SPLIT = 256
+EARLY_BLOCKS = 5
 
 
 def tile_attend_conditioned_runcap_delivered_kernel(
@@ -41,18 +50,32 @@ def tile_attend_conditioned_runcap_delivered_kernel(
         def bank(b):
             return psum.tile([P, BANK], F32, name=f"bank{b}")
 
+        def copy(engine, dst, src):
+            if engine == SCALAR:
+                nc.scalar.copy(out=dst, in_=src)
+            else:
+                nc.vector.tensor_copy(out=dst, in_=src)
+
+        def move(engine, dst, src):
+            if engine == SCALAR:
+                nc.scalar.activation(out=dst, in_=src, func=ACT.Copy)
+            else:
+                nc.vector.tensor_copy(out=dst, in_=src)
+
         key_scales = sb("key_scales", [P, T // 4], I32)
         nc.gpsimd.memset(key_scales[:], 0)
         query_raw = sb("query_raw", [P, PACK, Q])
         nc.sync.dma_start(out=query_raw[:], in_=query.rearrange("(p t) q -> p t q", t=PACK))
         scale_rows = keys_scales[0].bitcast(I32)
-        for u in range(4):
-            nc.sync.dma_start(out=key_scales[32 * u : 32 * u + 4, :], in_=scale_rows[4 * u : 4 * u + 4, :])
+        for quadrant in range(4):
+            nc.sync.dma_start(
+                out=key_scales[32 * quadrant : 32 * quadrant + 4, :], in_=scale_rows[4 * quadrant : 4 * quadrant + 4, :]
+            )
         key_words = sb("key_words", [P, 2 * T], U8)
         nc.sync.dma_start(out=key_words[:], in_=keys_words[0])
         lists = {}
         for name, src in (("second", offs3), ("judge", offs2), ("first", offs)):
-            lists[name] = keep.tile([P, I // 16], U16, name=f"list_{name}")
+            lists[name] = keep.tile([P, I // ENTRIES], U16, name=f"list_{name}")
             nc.sync.dma_start(lists[name][:], src)
         lam_cols = [sb(f"lam{r}", [P, 1]) for r in range(PACK)]
         with nc.allow_non_contiguous_dma(reason="one factor to a partition"):
@@ -64,38 +87,36 @@ def tile_attend_conditioned_runcap_delivered_kernel(
             nc.sync.dma_start(out=row_factor[name][:], in_=src.rearrange("(p r) o -> p (r o)", r=PACK))
         msgs_raw = sb("msgs_raw", [P, PACK, E])
         nc.sync.dma_start(out=msgs_raw[:], in_=msgs.rearrange("(p t) e -> p t e", t=PACK))
-        lists["places"] = keep.tile([P, I // 16], U16, name="list_places")
+        lists["places"] = keep.tile([P, I // ENTRIES], U16, name="list_places")
         nc.sync.dma_start(lists["places"][:], offs4)
-        old_tiles = [sb(f"old{j}", [P, M]) for j in range(4)]
-        for j in range(4):
-            nc.sync.dma_start(out=old_tiles[j][:], in_=old[j * P : (j + 1) * P, :])
-        fade_cols = sb("fade_cols", [P, M // P])
+        contents = [sb(f"old{j}", [P, M]) for j in range(TILES)]
+        for j in range(TILES):
+            nc.sync.dma_start(out=contents[j][:], in_=old[j * P : (j + 1) * P, :])
+        fade_cols = sb("fade_cols", [P, BLOCKS])
         with nc.allow_non_contiguous_dma(reason="one fading value to a partition"):
             nc.sync.dma_start(out=fade_cols[:], in_=fade.rearrange("o (b p) -> p (o b)", p=P))
 
-        windows = [sb(f"window{j}", [P, M]) for j in range(4)]
-        for j in range(4):
-            (nc.vector if j < 4 else nc.gpsimd).memset(windows[j][:], 0.0)
+        windows = [sb(f"window{j}", [P, M]) for j in range(TILES)]
+        for j in range(TILES):
+            nc.vector.memset(windows[j][:], 0.0)
         identity = sb("identity", [P, P])
         make_identity(nc, identity[:])
 
         query_codes = sb("query_codes", [P, Q], U32)
         query_scales = sb("query_scales", [P, Q], U8)
-        score_banks = {}
         query_dealt = query_raw[:].rearrange("p t (s r) -> p r s t", r=PACK)
+        product_banks = {}
+        products = {}
         for r in range(PACK):
             cols = slice(r * P, (r + 1) * P)
-            query_bf = sb(f"query_bf{r}", [P, P, PACK], BF16)
-            if r == 1:
-                nc.scalar.copy(out=query_bf[:], in_=query_dealt[:, r, :, :])
-            else:
-                nc.vector.tensor_copy(out=query_bf[:], in_=query_dealt[:, r, :, :])
+            query_bf = sb(f"query_bf{r}", [P, P, PACK], BF16, tag="query_bf0" if r == LAST else None)
+            copy(VECTOR if r in (0, LAST) else SCALAR, query_bf[:], query_dealt[:, r, :, :])
             nc.vector.quantize_mx(
                 out=query_codes[:, cols].bitcast(FP8X4),
                 scales=query_scales[:, cols],
                 in_=query_bf[:].rearrange("p s t -> p (s t)"),
             )
-            banks = (0, 1, 6, 7) if r == 0 else (2 * r, 2 * r + 1)
+            banks = (0, 1, 2 * LAST, 2 * LAST + 1) if r == 0 else (2 * r, 2 * r + 1)
             width = T // len(banks)
             for h, b in enumerate(banks):
                 acc = bank(b)
@@ -108,224 +129,148 @@ def tile_attend_conditioned_runcap_delivered_kernel(
                     start=True,
                     stop=True,
                 )
-                score_banks[r, h] = acc[:, :width]
+                product_banks[r, h] = acc[:, :width]
             if r == 0:
-                first_products = sb("products0", [P, T])
-                for h in range(4):
-                    dst = first_products[:, h * width : (h + 1) * width]
-                    if h % 2 == 0:
-                        nc.scalar.activation(out=dst, in_=score_banks[0, h], func=ACT.Copy)
-                    else:
-                        nc.vector.tensor_copy(out=dst, in_=score_banks[0, h])
+                products[0] = sb("products0", [P, T])
+                for h in range(len(banks)):
+                    move((SCALAR, VECTOR)[h % 2], products[0][:, h * width : (h + 1) * width], product_banks[0, h])
 
         cap_floor = sb("cap_floor", [P, PACK])
         cap_qs = sb("cap_qs", [P, PACK])
         weights_bf = sb("weights_bf", [P, PACK, I], BF16)
-        tiles = {("products", 0): first_products}
+        msgs_codes = [sb(f"msgs_codes{h}", [P, E // 2], U32) for h in range(2)]
+        msgs_scales = [sb(f"msgs_scales{h}", [P, E // 2], U8) for h in range(2)]
+        second, gate, mixed, neg_score, neg_max, expo, row_sum, divisor, inverse = {}, {}, {}, {}, {}, {}, {}, {}, {}
 
-        def empty_scores(r, h, engine, after=None):
-            if h == 0:
-                tiles["products", r] = sb(f"products{r}", [P, T], tag=f"score{r - 2}" if r >= 2 else None)
-            dst = tiles["products", r][:, h * BANK : (h + 1) * BANK]
-            if engine == "S":
-                nc.scalar.activation(out=dst, in_=score_banks[r, h], func=ACT.Copy)
-            else:
-                nc.vector.tensor_copy(out=dst, in_=score_banks[r, h])
+        def empty_products(r):
+            products[r] = sb(f"products{r}", [P, T], tag=f"score{r - 2}" if r >= 2 else None)
+            for h in range(2):
+                move(SCALAR, products[r][:, h * BANK : (h + 1) * BANK], product_banks[r, h])
 
-        def look_second(r, engine="S"):
-            tiles["second", r] = sb(f"second{r}", [P, I])
-            looked = tiles["products", r][:].indirect(lists["second"][:])
-            if engine == "S":
-                nc.scalar.activation(out=tiles["second", r][:], in_=looked, func=ACT.Copy)
-            else:
-                nc.vector.tensor_copy(out=tiles["second", r][:], in_=looked)
+        def look_up(r):
+            judge = sb(f"judge_product{r}", [P, I])
+            move(SCALAR, judge[:], products[r][:].indirect(lists["judge"][:]))
+            second[r] = sb(f"second{r}", [P, I])
+            move(VECTOR if r == 0 else SCALAR, second[r][:], products[r][:].indirect(lists["second"][:]))
+            gate[r] = sb(f"judge{r}", [P, I], tag=f"lam{r - 1}" if r >= 1 else None)
+            nc.scalar.activation(out=gate[r][:], in_=judge[:], func=ACT.Tanh)
 
-        def look_judge(r):
-            tiles["judge_product", r] = sb(f"judge_product{r}", [P, I])
-            nc.scalar.activation(
-                out=tiles["judge_product", r][:], in_=tiles["products", r][:].indirect(lists["judge"][:]), func=ACT.Copy
-            )
+        def row_constants():
+            nc.vector.tensor_scalar(out=cap_floor[:], in0=row_factor["cap"][:], scalar1=TINY, scalar2=None, op0=ALU.max)
+            nc.vector.tensor_tensor(out=cap_qs[:], in0=row_factor["cap"][:], in1=row_factor["qs"][:], op=ALU.mult)
 
-        def squash(r, after=None):
-            tiles["judge", r] = sb(f"judge{r}", [P, I], tag=f"lam{r - 1}" if r >= 1 else None)
-            nc.scalar.activation(out=tiles["judge", r][:], in_=tiles["judge_product", r][:], func=ACT.Tanh)
-
-        def difference(r, after=None):
-            tiles["mixed", r] = sb(f"mixed{r}", [P, I], tag="mixed")
+        def difference(r):
+            mixed[r] = sb(f"mixed{r}", [P, I], tag="mixed")
             nc.vector.tensor_tensor(
-                out=tiles["mixed", r][:], in0=tiles["products", r][:].indirect(lists["first"][:]),
-                in1=tiles["second", r][:], op=ALU.subtract,
+                out=mixed[r][:], in0=products[r][:].indirect(lists["first"][:]), in1=second[r][:], op=ALU.subtract
             )
 
-        def mix(r):
-            s = tiles["mixed", r]
+        def apply_gate(r):
             nc.vector.scalar_tensor_tensor(
-                out=s[:], in0=tiles["judge", r][:], scalar=1.0, in1=s[:], op0=ALU.add, op1=ALU.mult
+                out=mixed[r][:], in0=gate[r][:], scalar=1.0, in1=mixed[r][:], op0=ALU.add, op1=ALU.mult
             )
 
         def blend(r):
-            s = tiles["mixed", r]
             nc.vector.scalar_tensor_tensor(
-                out=s[:], in0=s[:], scalar=-0.5, in1=tiles["second", r][:], op0=ALU.mult, op1=ALU.subtract
+                out=mixed[r][:], in0=mixed[r][:], scalar=-0.5, in1=second[r][:], op0=ALU.mult, op1=ALU.subtract
             )
 
         def peak(r):
-            tiles["score", r] = sb(f"score{r}", [P, I])
-            tiles["neg_max", r] = sb(f"neg_max{r}", [P, 1])
+            neg_score[r] = sb(f"score{r}", [P, I])
+            neg_max[r] = sb(f"neg_max{r}", [P, 1])
             nc.vector.tensor_scalar(
-                out=tiles["score", r][:], in0=tiles["mixed", r][:], scalar1=lam_cols[r][:], scalar2=None,
-                op0=ALU.mult, op1=ALU.min, accum_out=tiles["neg_max", r][:],
+                out=neg_score[r][:], in0=mixed[r][:], scalar1=lam_cols[r][:], scalar2=None,
+                op0=ALU.mult, op1=ALU.min, accum_out=neg_max[r][:],
             )
 
-        def exponent(r):
-            tiles["p", r] = sb(f"p{r}", [P, G, RUN])
-            tiles["row_sum", r] = sb(f"row_sum{r}", [P, 1])
+        def exponential(r):
+            expo[r] = sb(f"p{r}", [P, G, RUN])
+            row_sum[r] = sb(f"row_sum{r}", [P, 1])
             nc.scalar.activation(
-                out=tiles["p", r][:].rearrange("p g j -> p (g j)"), in_=tiles["score", r][:], func=ACT.Exp,
-                bias=tiles["neg_max", r][:], scale=-1.0, accum_out=tiles["row_sum", r][:],
+                out=expo[r][:].rearrange("p g j -> p (g j)"), in_=neg_score[r][:], func=ACT.Exp,
+                bias=neg_max[r][:], scale=-1.0, accum_out=row_sum[r][:],
             )
 
-        def run_sums(r):
-            tiles["run_sum", r] = sb(f"run_sum{r}", [P, G])
-            nc.vector.tensor_reduce(out=tiles["run_sum", r][:], in_=tiles["p", r][:], axis=AXIS.X, op=ALU.add)
+        def sum_runs(r):
+            divisor[r] = sb(f"run_sum{r}", [P, G])
+            nc.vector.tensor_reduce(out=divisor[r][:], in_=expo[r][:], axis=AXIS.X, op=ALU.add)
 
-        def clamp(r):
-            run_sum = tiles["run_sum", r]
+        def apply_cap(r):
             nc.vector.scalar_tensor_tensor(
-                out=run_sum[:], in0=cap_floor[:, r : r + 1].to_broadcast([P, G]), scalar=tiles["row_sum", r][:],
-                in1=run_sum[:], op0=ALU.mult, op1=ALU.max,
+                out=divisor[r][:], in0=cap_floor[:, r : r + 1].to_broadcast([P, G]), scalar=row_sum[r][:],
+                in1=divisor[r][:], op0=ALU.mult, op1=ALU.max,
             )
 
-        def invert(r, slots=slice(0, I)):
-            if slots.start == 0:
-                tiles["inverse", r] = sb(f"inverse{r}", [P, G])
-            runs = slice(slots.start // RUN, slots.stop // RUN)
-            nc.vector.reciprocal(out=tiles["inverse", r][:, runs], in_=tiles["run_sum", r][:, runs])
+        def runs_in_pieces(r):
+            pieces = PIECES if r == LAST else (slice(0, I),)
+            return [(slots, slice(slots.start // RUN, slots.stop // RUN)) for slots in pieces]
 
-        def final(r, slots=slice(0, I)):
-            runs = slice(slots.start // RUN, slots.stop // RUN)
-            count = runs.stop - runs.start
-            nc.vector.scalar_tensor_tensor(
-                out=weights_bf[:, r, slots].rearrange("p (g j) -> p g j", j=RUN), in0=tiles["p", r][:, runs, :],
-                scalar=cap_qs[:, r : r + 1],
-                in1=tiles["inverse", r][:, runs].unsqueeze(2).to_broadcast([P, count, RUN]), op0=ALU.mult, op1=ALU.mult,
-            )
+        def invert(r):
+            inverse[r] = sb(f"inverse{r}", [P, G])
+            for slots, runs in runs_in_pieces(r):
+                nc.vector.reciprocal(out=inverse[r][:, runs], in_=divisor[r][:, runs])
 
-        msgs_codes = [sb(f"msgs_codes{h}", [P, E // 2], U32) for h in range(2)]
-        msgs_scales = [sb(f"msgs_scales{h}", [P, E // 2], U8) for h in range(2)]
+        def weigh(r):
+            for slots, runs in runs_in_pieces(r):
+                nc.vector.scalar_tensor_tensor(
+                    out=weights_bf[:, r, slots].rearrange("p (g j) -> p g j", j=RUN), in0=expo[r][:, runs, :],
+                    scalar=cap_qs[:, r : r + 1],
+                    in1=inverse[r][:, runs].unsqueeze(2).to_broadcast([P, runs.stop - runs.start, RUN]),
+                    op0=ALU.mult, op1=ALU.mult,
+                )
 
-        def weave_msgs(h, after=None):
-            tiles["msgs_bf", h] = sb(f"msgs_bf{h}", [P, E // 2, PACK], BF16, tag=("score2", "neg_max3")[h])
+        score_steps = (difference, apply_gate, blend, peak)
+        weight_steps = (sum_runs, apply_cap, invert, weigh)
+        for r in range(PACK + 1):
+            if r < PACK:
+                if r > 0:
+                    empty_products(r)
+                look_up(r)
+            if r == 0:
+                row_constants()
+            for score_step, weight_step in zip(score_steps, weight_steps):
+                if r < PACK:
+                    score_step(r)
+                if r > 0:
+                    weight_step(r - 1)
+            if r < PACK:
+                exponential(r)
+
+        for h, tag in enumerate((f"score{LAST - 1}", f"neg_max{LAST}")):
+            msgs_bf = sb(f"msgs_bf{h}", [P, E // 2, PACK], BF16, tag=tag)
             nc.scalar.copy(
-                out=tiles["msgs_bf", h][:].rearrange("p (c i) t -> p c t i", i=4),
-                in_=msgs_raw[:, :, h * (E // 2) : (h + 1) * (E // 2)].rearrange("p t (c i) -> p c t i", i=4),
+                out=msgs_bf[:].rearrange("p (c i) t -> p c t i", i=LINE),
+                in_=msgs_raw[:, :, h * (E // 2) : (h + 1) * (E // 2)].rearrange("p t (c i) -> p c t i", i=LINE),
             )
-
-        def quantize_msgs(h):
             nc.vector.quantize_mx(
-                out=msgs_codes[h][:].bitcast(FP8X4), scales=msgs_scales[h][:],
-                in_=tiles["msgs_bf", h][:].rearrange("p e t -> p (e t)"),
+                out=msgs_codes[h][:].bitcast(FP8X4), scales=msgs_scales[h][:], in_=msgs_bf[:].rearrange("p e t -> p (e t)")
             )
 
-        def row_constants():
-            nc.vector.tensor_scalar(
-                out=cap_floor[:], in0=row_factor["cap"][:], scalar1=TINY, scalar2=None, op0=ALU.max
-            )
-            nc.vector.tensor_tensor(out=cap_qs[:], in0=row_factor["cap"][:], in1=row_factor["qs"][:], op=ALU.mult)
-
-        def fade_turned(b, after=None):
-            if b == 0:
-                early = sb("faded_early", [P, EARLY, E], tag="judge_product3")
-                late = sb("faded_late", [P, M // P - EARLY, E], tag="score3")
-                tiles["faded"] = [early[:, k, :] for k in range(EARLY)] + [late[:, k, :] for k in range(M // P - EARLY)]
+        early = sb("faded_early", [P, EARLY_BLOCKS, E], tag=f"judge_product{LAST}")
+        late = sb("faded_late", [P, BLOCKS - EARLY_BLOCKS, E], tag=f"score{LAST}")
+        faded = [early[:, b, :] for b in range(EARLY_BLOCKS)] + [late[:, b, :] for b in range(BLOCKS - EARLY_BLOCKS)]
+        for b in range(BLOCKS):
             turned = bank(b)
-            for j in range(4):
-                nc.tensor.transpose(turned[:, j * P : (j + 1) * P], old_tiles[j][:, b * P : (b + 1) * P], identity[:])
-            nc.scalar.activation(out=tiles["faded"][b], in_=turned[:], func=ACT.Copy, scale=fade_cols[:, b : b + 1])
-
-        look_judge(0)
-        look_second(0, "V")
-        squash(0)
-        row_constants()
-        difference(0)
-        mix(0)
-        blend(0)
-        peak(0)
-        exponent(0)
-        empty_scores(1, 0, "S")
-        empty_scores(1, 1, "S")
-        look_judge(1)
-        look_second(1)
-        squash(1, "m0")
-        difference(1, "m0")
-        run_sums(0)
-        mix(1)
-        clamp(0)
-        blend(1)
-        invert(0)
-        peak(1)
-        final(0)
-        exponent(1)
-        empty_scores(2, 0, "S", "x0")
-        empty_scores(2, 1, "S", "x0")
-        look_judge(2)
-        look_second(2)
-        squash(2, "m1")
-        difference(2, "m1")
-        run_sums(1)
-        mix(2)
-        clamp(1)
-        blend(2)
-        invert(1)
-        peak(2)
-        final(1)
-        exponent(2)
-        empty_scores(3, 0, "S", "x1")
-        empty_scores(3, 1, "S", "x1")
-        look_judge(3)
-        look_second(3)
-        squash(3, "m2")
-        difference(3, "m2")
-        run_sums(2)
-        mix(3)
-        clamp(2)
-        blend(3)
-        invert(2)
-        peak(3)
-        final(2)
-        exponent(3)
-        run_sums(3)
-        clamp(3)
-        invert(3, PIECES[0])
-        invert(3, PIECES[1])
-        final(3, PIECES[0])
-        final(3, PIECES[1])
-        weave_msgs(0, "x2")
-        quantize_msgs(0)
-        weave_msgs(1, "x3")
-        quantize_msgs(1)
-        fade_turned(0, "t3")
-        fade_turned(1, "t3")
-        fade_turned(2, "t3")
-        fade_turned(3, "t3")
-        fade_turned(4, "t3")
-        fade_turned(5, "x3")
-        fade_turned(6, "x3")
-        fade_turned(7, "x3")
+            for j in range(TILES):
+                nc.tensor.transpose(turned[:, j * P : (j + 1) * P], contents[j][:, b * P : (b + 1) * P], identity[:])
+            nc.scalar.activation(out=faded[b], in_=turned[:], func=ACT.Copy, scale=fade_cols[:, b : b + 1])
 
         widths = [piece.stop - piece.start for piece in PIECES]
-        woven = [sb(f"woven{h}", [P, widths[h], PACK], BF16) for h in range(2)]
-        weight_codes = [sb(f"weight_codes{h}", [P, widths[h]], U32) for h in range(2)]
-        weight_scales = [sb(f"weight_scales{h}", [P, widths[h]], U8) for h in range(2)]
-        for h, lo, hi, engine in ((0, 0, 128, "V"), (1, 128, 256, "V"), (1, 256, I, "S")):
+        woven = [sb(f"woven{h}", [P, widths[h], PACK], BF16) for h in (SHORT, LONG)]
+        weight_codes = [sb(f"weight_codes{h}", [P, widths[h]], U32) for h in (SHORT, LONG)]
+        weight_scales = [sb(f"weight_scales{h}", [P, widths[h]], U8) for h in (SHORT, LONG)]
+        for h, lo, hi, engine in (
+            (SHORT, PIECES[SHORT].start, PIECES[SHORT].stop, VECTOR),
+            (LONG, PIECES[LONG].start, WEAVE_SPLIT, VECTOR),
+            (LONG, WEAVE_SPLIT, PIECES[LONG].stop, SCALAR),
+        ):
             base = PIECES[h].start
-            dst = woven[h][:, lo - base : hi - base, :].rearrange("p (c i) r -> p c r i", i=4)
-            src = weights_bf[:, :, lo:hi].rearrange("p r (c i) -> p c r i", i=4)
-            if engine == "V":
-                nc.vector.tensor_copy(out=dst, in_=src)
-            else:
-                nc.scalar.copy(out=dst, in_=src)
-        sums = {}
+            copy(
+                engine,
+                woven[h][:, lo - base : hi - base, :].rearrange("p (c i) r -> p c r i", i=LINE),
+                weights_bf[:, :, lo:hi].rearrange("p r (c i) -> p c r i", i=LINE),
+            )
+        sums, staged = {}, {}
 
         def quantize_weights(h):
             nc.vector.quantize_mx(
@@ -333,80 +278,66 @@ def tile_attend_conditioned_runcap_delivered_kernel(
                 in_=woven[h][:].rearrange("p i r -> p (i r)"),
             )
 
-        def multiply(j, h, b):
-            acc = bank(b)
-            cols = slice((j % 2) * P, (j % 2 + 1) * P)
-            for part_cols in ((slice(0, 128),), (slice(0, 128), slice(128, 384)))[h]:
+        def multiply(j, h):
+            acc = bank(TILES + j)
+            features = slice((j % 2) * P, (j % 2 + 1) * P)
+            for slots in (slice(0, 128),) if h == SHORT else (slice(0, 128), slice(128, 384)):
                 nc.tensor.matmul_mx(
-                    out=acc[:, part_cols],
-                    lhsT=msgs_codes[j // 2][:, cols].bitcast(FP8X4),
-                    lhsT_scale=msgs_scales[j // 2][:, cols],
-                    rhs=weight_codes[h][:, part_cols].bitcast(FP8X4),
-                    rhs_scale=weight_scales[h][:, part_cols],
+                    out=acc[:, slots],
+                    lhsT=msgs_codes[j // 2][:, features].bitcast(FP8X4),
+                    lhsT_scale=msgs_scales[j // 2][:, features],
+                    rhs=weight_codes[h][:, slots].bitcast(FP8X4),
+                    rhs_scale=weight_scales[h][:, slots],
                     start=True,
                     stop=True,
                 )
             sums[j, h] = acc
 
         def stage(j, h, engine):
-            tiles["staged", j, h] = sb(f"staged{j}_{h}", [P, widths[h]])
-            if engine == "S":
-                nc.scalar.copy(out=tiles["staged", j, h][:], in_=sums[j, h][:, : widths[h]])
-            else:
-                nc.vector.tensor_copy(out=tiles["staged", j, h][:], in_=sums[j, h][:, : widths[h]])
+            staged[j, h] = sb(f"staged{j}_{h}", [P, widths[h]])
+            copy(engine, staged[j, h][:], sums[j, h][:, : widths[h]])
 
         def scatter(j, h, engine):
-            places = windows[j][:].indirect(lists["places"][:, PIECES[h].start // 16 : PIECES[h].stop // 16])
-            if engine == "S":
-                nc.scalar.activation(out=places, in_=tiles["staged", j, h][:], func=ACT.Copy)
-            else:
-                nc.vector.tensor_copy(out=places, in_=tiles["staged", j, h][:])
+            entries = lists["places"][:, PIECES[h].start // ENTRIES : PIECES[h].stop // ENTRIES]
+            move(engine, windows[j][:].indirect(entries), staged[j, h][:])
 
-        def finish(j, k, b, pieces=1):
-            back = bank(b)
-            for c in range(4):
+        def finish(j, half, stores):
+            back = bank(TILES * half + j)
+            for c in range(BANK // P):
                 nc.tensor.transpose(
-                    back[:, c * P : (c + 1) * P], tiles["faded"][4 * k + c][:, j * P : (j + 1) * P], identity[:]
+                    back[:, c * P : (c + 1) * P], faded[(BANK // P) * half + c][:, j * P : (j + 1) * P], identity[:]
                 )
-            width = BANK // pieces
-            for n in range(pieces):
-                cols = slice(k * BANK + n * width, k * BANK + (n + 1) * width)
+            width = BANK // stores
+            for n in range(stores):
+                cols = slice(half * BANK + n * width, half * BANK + (n + 1) * width)
                 nc.vector.tensor_tensor(
-                    out=old_tiles[j][:, cols], in0=back[:, n * width : (n + 1) * width], in1=windows[j][:, cols], op=ALU.add
+                    out=contents[j][:, cols], in0=back[:, n * width : (n + 1) * width], in1=windows[j][:, cols], op=ALU.add
                 )
-                nc.sync.dma_start(out=out[j * P : (j + 1) * P, cols], in_=old_tiles[j][:, cols])
+                nc.sync.dma_start(out=out[j * P : (j + 1) * P, cols], in_=contents[j][:, cols])
 
-        quantize_weights(0)
-        multiply(0, 0, 4)
-        multiply(1, 0, 5)
-        multiply(2, 0, 6)
-        stage(0, 0, "V")
-        scatter(0, 0, "S")
-        quantize_weights(1)
-        stage(1, 0, "V")
-        stage(2, 0, "V")
-        multiply(0, 1, 4)
-        multiply(3, 1, 7)
-        multiply(1, 1, 5)
-        multiply(2, 1, 6)
-        scatter(1, 0, "S")
-        stage(0, 1, "V")
-        scatter(0, 1, "S")
-        scatter(2, 0, "V")
-        stage(3, 1, "V")
-        multiply(3, 0, 7)
-        stage(1, 1, "V")
-        stage(3, 0, "V")
-        scatter(3, 1, "V")
-        scatter(3, 0, "V")
-        scatter(1, 1, "S")
-        stage(2, 1, "S")
-        scatter(2, 1, "S")
-        finish(0, 0, 0)
-        finish(0, 1, 4)
-        finish(3, 0, 3)
-        finish(3, 1, 7)
-        finish(1, 0, 1)
-        finish(1, 1, 5)
-        finish(2, 0, 2)
-        finish(2, 1, 6, 2)
+        quantize_weights(SHORT)
+        for j in (0, 1, 2):
+            multiply(j, SHORT)
+        stage(0, SHORT, VECTOR)
+        scatter(0, SHORT, SCALAR)
+        quantize_weights(LONG)
+        for j in (1, 2):
+            stage(j, SHORT, VECTOR)
+        for j in (0, 3, 1, 2):
+            multiply(j, LONG)
+        scatter(1, SHORT, SCALAR)
+        stage(0, LONG, VECTOR)
+        scatter(0, LONG, SCALAR)
+        scatter(2, SHORT, VECTOR)
+        stage(3, LONG, VECTOR)
+        multiply(3, SHORT)
+        stage(1, LONG, VECTOR)
+        stage(3, SHORT, VECTOR)
+        scatter(3, LONG, VECTOR)
+        scatter(3, SHORT, VECTOR)
+        scatter(1, LONG, SCALAR)
+        stage(2, LONG, SCALAR)
+        scatter(2, LONG, SCALAR)
+        finishing = [(j, half) for j in (0, 3, 1, 2) for half in range(2)]
+        for j, half in finishing:
+            finish(j, half, 2 if (j, half) == finishing[-1] else 1)

from contextlib import ExitStack

import concourse.mybir as mybir
from concourse.masks import make_identity

D, T, I, Q, E, G, M = 512, 1024, 512, 512, 512, 64, 1024
FLOPS = 2 * D * Q * T + 2 * Q * E * I

F32 = mybir.dt.float32
BF16 = mybir.dt.bfloat16
I32 = mybir.dt.int32
U32 = mybir.dt.uint32
U16 = mybir.dt.uint16
U8 = mybir.dt.uint8
FP8X4 = mybir.dt.float8_e4m3fn_x4
FP4X4 = mybir.dt.float4_e2m1fn_x4
ALU = mybir.AluOpType
ACT = mybir.ActivationFunctionType
AXIS = mybir.AxisListType

P = 128
SCALAR, VECTOR = "scalar", "vector"
PACK = 4
BANK = 512
RUN = I // G
TILES = E // P
BLOCKS = M // P
LAST = PACK - 1
LINE = 4
ENTRIES = 16
TINY = 1e-30

SHORT, LONG = 0, 1
PIECES = (slice(0, 128), slice(128, I))
WEAVE_SPLIT = 256
EARLY_BLOCKS = 5


def tile_attend_conditioned_runcap_delivered_kernel(
    tc, query, keys_words, keys_scales, lam, cap, qs, msgs, old, fade, offs, offs2, offs3, offs4, out
):
    nc = tc.nc
    with ExitStack() as ctx:
        keep = ctx.enter_context(tc.tile_pool(name="keep", bufs=1))
        psum = ctx.enter_context(tc.psum_pool(name="psum", bufs=1))

        def sb(name, shape, dtype=F32, tag=None):
            return keep.tile(shape, dtype, name=name, tag=tag or name, align_bytes=64)

        def bank(b):
            return psum.tile([P, BANK], F32, name=f"bank{b}")

        def copy(engine, dst, src):
            if engine == SCALAR:
                nc.scalar.copy(out=dst, in_=src)
            else:
                nc.vector.tensor_copy(out=dst, in_=src)

        def move(engine, dst, src):
            if engine == SCALAR:
                nc.scalar.activation(out=dst, in_=src, func=ACT.Copy)
            else:
                nc.vector.tensor_copy(out=dst, in_=src)

        key_scales = sb("key_scales", [P, T // 4], I32)
        nc.gpsimd.memset(key_scales[:], 0)
        query_raw = sb("query_raw", [P, PACK, Q])
        nc.sync.dma_start(out=query_raw[:], in_=query.rearrange("(p t) q -> p t q", t=PACK))
        scale_rows = keys_scales[0].bitcast(I32)
        for quadrant in range(4):
            nc.sync.dma_start(
                out=key_scales[32 * quadrant : 32 * quadrant + 4, :], in_=scale_rows[4 * quadrant : 4 * quadrant + 4, :]
            )
        key_words = sb("key_words", [P, 2 * T], U8)
        nc.sync.dma_start(out=key_words[:], in_=keys_words[0])
        lists = {}
        for name, src in (("second", offs3), ("judge", offs2), ("first", offs)):
            lists[name] = keep.tile([P, I // ENTRIES], U16, name=f"list_{name}")
            nc.sync.dma_start(lists[name][:], src)
        lam_cols = [sb(f"lam{r}", [P, 1]) for r in range(PACK)]
        with nc.allow_non_contiguous_dma(reason="one factor to a partition"):
            for r in range(PACK):
                nc.sync.dma_start(out=lam_cols[r][:], in_=lam.rearrange("(p r) o -> r p o", r=PACK)[r])
        row_factor = {}
        for name, src in (("cap", cap), ("qs", qs)):
            row_factor[name] = sb(f"row_{name}", [P, PACK])
            nc.sync.dma_start(out=row_factor[name][:], in_=src.rearrange("(p r) o -> p (r o)", r=PACK))
        msgs_raw = sb("msgs_raw", [P, PACK, E])
        nc.sync.dma_start(out=msgs_raw[:], in_=msgs.rearrange("(p t) e -> p t e", t=PACK))
        lists["places"] = keep.tile([P, I // ENTRIES], U16, name="list_places")
        nc.sync.dma_start(lists["places"][:], offs4)
        contents = [sb(f"old{j}", [P, M]) for j in range(TILES)]
        for j in range(TILES):
            nc.sync.dma_start(out=contents[j][:], in_=old[j * P : (j + 1) * P, :])
        fade_cols = sb("fade_cols", [P, BLOCKS])
        with nc.allow_non_contiguous_dma(reason="one fading value to a partition"):
            nc.sync.dma_start(out=fade_cols[:], in_=fade.rearrange("o (b p) -> p (o b)", p=P))

        windows = [sb(f"window{j}", [P, M]) for j in range(TILES)]
        for j in range(TILES):
            nc.vector.memset(windows[j][:], 0.0)
        identity = sb("identity", [P, P])
        make_identity(nc, identity[:])

        query_codes = sb("query_codes", [P, Q], U32)
        query_scales = sb("query_scales", [P, Q], U8)
        query_dealt = query_raw[:].rearrange("p t (s r) -> p r s t", r=PACK)
        product_banks = {}
        products = {}
        for r in range(PACK):
            cols = slice(r * P, (r + 1) * P)
            query_bf = sb(f"query_bf{r}", [P, P, PACK], BF16, tag="query_bf0" if r == LAST else None)
            copy(VECTOR if r in (0, LAST) else SCALAR, query_bf[:], query_dealt[:, r, :, :])
            nc.vector.quantize_mx(
                out=query_codes[:, cols].bitcast(FP8X4),
                scales=query_scales[:, cols],
                in_=query_bf[:].rearrange("p s t -> p (s t)"),
            )
            banks = (0, 1, 2 * LAST, 2 * LAST + 1) if r == 0 else (2 * r, 2 * r + 1)
            width = T // len(banks)
            for h, b in enumerate(banks):
                acc = bank(b)
                nc.tensor.matmul_mx(
                    out=acc[:, :width],
                    lhsT=query_codes[:, cols].bitcast(FP8X4),
                    lhsT_scale=query_scales[:, cols],
                    rhs=key_words[:, h * 2 * width : (h + 1) * 2 * width].bitcast(FP4X4),
                    rhs_scale=key_scales[:].bitcast(U8)[:, h * width : (h + 1) * width],
                    start=True,
                    stop=True,
                )
                product_banks[r, h] = acc[:, :width]
            if r == 0:
                products[0] = sb("products0", [P, T])
                for h in range(len(banks)):
                    move((SCALAR, VECTOR)[h % 2], products[0][:, h * width : (h + 1) * width], product_banks[0, h])

        cap_floor = sb("cap_floor", [P, PACK])
        cap_qs = sb("cap_qs", [P, PACK])
        weights_bf = sb("weights_bf", [P, PACK, I], BF16)
        msgs_codes = [sb(f"msgs_codes{h}", [P, E // 2], U32) for h in range(2)]
        msgs_scales = [sb(f"msgs_scales{h}", [P, E // 2], U8) for h in range(2)]
        second, gate, mixed, neg_score, neg_max, expo, row_sum, divisor, inverse = {}, {}, {}, {}, {}, {}, {}, {}, {}

        def empty_products(r):
            products[r] = sb(f"products{r}", [P, T], tag=f"score{r - 2}" if r >= 2 else None)
            for h in range(2):
                move(SCALAR, products[r][:, h * BANK : (h + 1) * BANK], product_banks[r, h])

        def look_up(r):
            judge = sb(f"judge_product{r}", [P, I])
            move(SCALAR, judge[:], products[r][:].indirect(lists["judge"][:]))
            second[r] = sb(f"second{r}", [P, I])
            move(VECTOR if r == 0 else SCALAR, second[r][:], products[r][:].indirect(lists["second"][:]))
            gate[r] = sb(f"judge{r}", [P, I], tag=f"lam{r - 1}" if r >= 1 else None)
            nc.scalar.activation(out=gate[r][:], in_=judge[:], func=ACT.Tanh)

        def row_constants():
            nc.vector.tensor_scalar(out=cap_floor[:], in0=row_factor["cap"][:], scalar1=TINY, scalar2=None, op0=ALU.max)
            nc.vector.tensor_tensor(out=cap_qs[:], in0=row_factor["cap"][:], in1=row_factor["qs"][:], op=ALU.mult)

        def difference(r):
            mixed[r] = sb(f"mixed{r}", [P, I], tag="mixed")
            nc.vector.tensor_tensor(
                out=mixed[r][:], in0=products[r][:].indirect(lists["first"][:]), in1=second[r][:], op=ALU.subtract
            )

        def apply_gate(r):
            nc.vector.scalar_tensor_tensor(
                out=mixed[r][:], in0=gate[r][:], scalar=1.0, in1=mixed[r][:], op0=ALU.add, op1=ALU.mult
            )

        def blend(r):
            nc.vector.scalar_tensor_tensor(
                out=mixed[r][:], in0=mixed[r][:], scalar=-0.5, in1=second[r][:], op0=ALU.mult, op1=ALU.subtract
            )

        def peak(r):
            neg_score[r] = sb(f"score{r}", [P, I])
            neg_max[r] = sb(f"neg_max{r}", [P, 1])
            nc.vector.tensor_scalar(
                out=neg_score[r][:], in0=mixed[r][:], scalar1=lam_cols[r][:], scalar2=None,
                op0=ALU.mult, op1=ALU.min, accum_out=neg_max[r][:],
            )

        def exponential(r):
            expo[r] = sb(f"p{r}", [P, G, RUN])
            row_sum[r] = sb(f"row_sum{r}", [P, 1])
            nc.scalar.activation(
                out=expo[r][:].rearrange("p g j -> p (g j)"), in_=neg_score[r][:], func=ACT.Exp,
                bias=neg_max[r][:], scale=-1.0, accum_out=row_sum[r][:],
            )

        def sum_runs(r):
            divisor[r] = sb(f"run_sum{r}", [P, G])
            nc.vector.tensor_reduce(out=divisor[r][:], in_=expo[r][:], axis=AXIS.X, op=ALU.add)

        def apply_cap(r):
            nc.vector.scalar_tensor_tensor(
                out=divisor[r][:], in0=cap_floor[:, r : r + 1].to_broadcast([P, G]), scalar=row_sum[r][:],
                in1=divisor[r][:], op0=ALU.mult, op1=ALU.max,
            )

        def runs_in_pieces(r):
            pieces = PIECES if r == LAST else (slice(0, I),)
            return [(slots, slice(slots.start // RUN, slots.stop // RUN)) for slots in pieces]

        def invert(r):
            inverse[r] = sb(f"inverse{r}", [P, G])
            for slots, runs in runs_in_pieces(r):
                nc.vector.reciprocal(out=inverse[r][:, runs], in_=divisor[r][:, runs])

        def weigh(r):
            for slots, runs in runs_in_pieces(r):
                nc.vector.scalar_tensor_tensor(
                    out=weights_bf[:, r, slots].rearrange("p (g j) -> p g j", j=RUN), in0=expo[r][:, runs, :],
                    scalar=cap_qs[:, r : r + 1],
                    in1=inverse[r][:, runs].unsqueeze(2).to_broadcast([P, runs.stop - runs.start, RUN]),
                    op0=ALU.mult, op1=ALU.mult,
                )

        score_steps = (difference, apply_gate, blend, peak)
        weight_steps = (sum_runs, apply_cap, invert, weigh)
        for r in range(PACK + 1):
            if r < PACK:
                if r > 0:
                    empty_products(r)
                look_up(r)
            if r == 0:
                row_constants()
            for score_step, weight_step in zip(score_steps, weight_steps):
                if r < PACK:
                    score_step(r)
                if r > 0:
                    weight_step(r - 1)
            if r < PACK:
                exponential(r)

        for h, tag in enumerate((f"score{LAST - 1}", f"neg_max{LAST}")):
            msgs_bf = sb(f"msgs_bf{h}", [P, E // 2, PACK], BF16, tag=tag)
            nc.scalar.copy(
                out=msgs_bf[:].rearrange("p (c i) t -> p c t i", i=LINE),
                in_=msgs_raw[:, :, h * (E // 2) : (h + 1) * (E // 2)].rearrange("p t (c i) -> p c t i", i=LINE),
            )
            nc.vector.quantize_mx(
                out=msgs_codes[h][:].bitcast(FP8X4), scales=msgs_scales[h][:], in_=msgs_bf[:].rearrange("p e t -> p (e t)")
            )

        early = sb("faded_early", [P, EARLY_BLOCKS, E], tag=f"judge_product{LAST}")
        late = sb("faded_late", [P, BLOCKS - EARLY_BLOCKS, E], tag=f"score{LAST}")
        faded = [early[:, b, :] for b in range(EARLY_BLOCKS)] + [late[:, b, :] for b in range(BLOCKS - EARLY_BLOCKS)]
        for b in range(BLOCKS):
            turned = bank(b)
            for j in range(TILES):
                nc.tensor.transpose(turned[:, j * P : (j + 1) * P], contents[j][:, b * P : (b + 1) * P], identity[:])
            nc.scalar.activation(out=faded[b], in_=turned[:], func=ACT.Copy, scale=fade_cols[:, b : b + 1])

        widths = [piece.stop - piece.start for piece in PIECES]
        woven = [sb(f"woven{h}", [P, widths[h], PACK], BF16) for h in (SHORT, LONG)]
        weight_codes = [sb(f"weight_codes{h}", [P, widths[h]], U32) for h in (SHORT, LONG)]
        weight_scales = [sb(f"weight_scales{h}", [P, widths[h]], U8) for h in (SHORT, LONG)]
        for h, lo, hi, engine in (
            (SHORT, PIECES[SHORT].start, PIECES[SHORT].stop, VECTOR),
            (LONG, PIECES[LONG].start, WEAVE_SPLIT, VECTOR),
            (LONG, WEAVE_SPLIT, PIECES[LONG].stop, SCALAR),
        ):
            base = PIECES[h].start
            copy(
                engine,
                woven[h][:, lo - base : hi - base, :].rearrange("p (c i) r -> p c r i", i=LINE),
                weights_bf[:, :, lo:hi].rearrange("p r (c i) -> p c r i", i=LINE),
            )
        sums, staged = {}, {}

        def quantize_weights(h):
            nc.vector.quantize_mx(
                out=weight_codes[h][:].bitcast(FP8X4), scales=weight_scales[h][:],
                in_=woven[h][:].rearrange("p i r -> p (i r)"),
            )

        def multiply(j, h):
            acc = bank(TILES + j)
            features = slice((j % 2) * P, (j % 2 + 1) * P)
            for slots in (slice(0, 128),) if h == SHORT else (slice(0, 128), slice(128, 384)):
                nc.tensor.matmul_mx(
                    out=acc[:, slots],
                    lhsT=msgs_codes[j // 2][:, features].bitcast(FP8X4),
                    lhsT_scale=msgs_scales[j // 2][:, features],
                    rhs=weight_codes[h][:, slots].bitcast(FP8X4),
                    rhs_scale=weight_scales[h][:, slots],
                    start=True,
                    stop=True,
                )
            sums[j, h] = acc

        def stage(j, h, engine):
            staged[j, h] = sb(f"staged{j}_{h}", [P, widths[h]])
            copy(engine, staged[j, h][:], sums[j, h][:, : widths[h]])

        def scatter(j, h, engine):
            entries = lists["places"][:, PIECES[h].start // ENTRIES : PIECES[h].stop // ENTRIES]
            move(engine, windows[j][:].indirect(entries), staged[j, h][:])

        def finish(j, half, stores):
            back = bank(TILES * half + j)
            for c in range(BANK // P):
                nc.tensor.transpose(
                    back[:, c * P : (c + 1) * P], faded[(BANK // P) * half + c][:, j * P : (j + 1) * P], identity[:]
                )
            width = BANK // stores
            for n in range(stores):
                cols = slice(half * BANK + n * width, half * BANK + (n + 1) * width)
                nc.vector.tensor_tensor(
                    out=contents[j][:, cols], in0=back[:, n * width : (n + 1) * width], in1=windows[j][:, cols], op=ALU.add
                )
                nc.sync.dma_start(out=out[j * P : (j + 1) * P, cols], in_=contents[j][:, cols])

        quantize_weights(SHORT)
        for j in (0, 1, 2):
            multiply(j, SHORT)
        stage(0, SHORT, VECTOR)
        scatter(0, SHORT, SCALAR)
        quantize_weights(LONG)
        for j in (1, 2):
            stage(j, SHORT, VECTOR)
        for j in (0, 3, 1, 2):
            multiply(j, LONG)
        scatter(1, SHORT, SCALAR)
        stage(0, LONG, VECTOR)
        scatter(0, LONG, SCALAR)
        scatter(2, SHORT, VECTOR)
        stage(3, LONG, VECTOR)
        multiply(3, SHORT)
        stage(1, LONG, VECTOR)
        stage(3, SHORT, VECTOR)
        scatter(3, LONG, VECTOR)
        scatter(3, SHORT, VECTOR)
        scatter(1, LONG, SCALAR)
        stage(2, LONG, SCALAR)
        scatter(2, LONG, SCALAR)
        finishing = [(j, half) for j in (0, 3, 1, 2) for half in range(2)]
        for j, half in finishing:
            finish(j, half, 2 if (j, half) == finishing[-1] else 1)
